import numpy as np, ml_dtypes
CORES = [40,64,80,88,96,104,120,144]
N = 8
import mx_ref
BF = ml_dtypes.bfloat16
def gentries(a):
    return np.ascontiguousarray(a.reshape(8, 16, -1).transpose(0, 2, 1)).reshape(8, -1)
def gtable(e):
    e = np.asarray(e); return np.ascontiguousarray(e.reshape(8, -1, 16).transpose(0, 2, 1)).reshape(128, -1).astype(np.int32)
def gcols(t, e):
    v = np.concatenate([t.reshape(8, 16, -1, 4), np.zeros((8, 16, 1, 4), BF)], axis=2)
    return np.ascontiguousarray(np.stack([v[g][:, e[g]] for g in range(8)])).reshape(128, -1)
def tile(rs):
    return np.stack(rs, axis=2).reshape(128, -1).astype(BF)
def pick(q, e):
    c = np.concatenate([q[0].reshape(128, -1, 4), np.zeros((128, 1, 4), np.uint8)], axis=1); s = np.concatenate([q[1], np.ones((16, 1), np.uint8)], axis=1)
    return (np.ascontiguousarray(c[:, e].reshape(128, -1)), np.ascontiguousarray(s[:, e]))
def join(*qs):
    return (np.concatenate([q[0] for q in qs], axis=1), np.concatenate([q[1] for q in qs], axis=1))
def put(q, e, v):
    c, s = q[0].reshape(128, -1, 4).copy(), q[1].copy(); c[:, e] = v[0].reshape(128, -1, 4); s[:, e] = v[1]
    return (c.reshape(128, -1), s)
def pk(c, s):
    return (np.ascontiguousarray(c), mx_ref.live(s))
def emit(q):
    return q[0], q[1]
def packed(v, rng):
    q = [mx_ref.quantize(np.ascontiguousarray(v[r])) for r in range(N)]
    return np.stack([a for a, b in q]), np.stack([mx_ref.plane(b, rng) for a, b in q])
def values_of_codes():
    e, c = np.zeros((128, 128, 4), np.float32), np.zeros((128, 2, 4), np.uint8)
    e[np.arange(128), np.arange(128), 0] = 1
    c[:127, :, 0] = np.arange(256).reshape(2, 128).T[:127]
    return mx_ref.matmul(mx_ref.quantize(e.reshape(128, 512).astype(BF)), (c.reshape(128, 8), np.full((16, 2), 127, np.uint8))).T.reshape(-1).astype(np.float64)
CODE_VALUE, SCALE_VALUE = values_of_codes(), 2.0 ** (np.arange(256) - 127.0)
def decode(q):
    return (CODE_VALUE[q[0]].reshape(16, 8, -1, 4) * SCALE_VALUE[q[1]][:, None, :, None] + 0.0).reshape(128, -1).astype(np.float32)
def f(rng, *shape):
    return mx_ref.flush((rng.standard_normal(shape, dtype=np.float32) * np.exp2(rng.integers(-2, 3, shape[:-1] + (1,)))).astype(BF))
def wide(rng, *shape, cols=0):
    v = rng.standard_normal(shape, dtype=np.float32) * np.exp2(rng.integers(-12, 13, shape)).astype(np.float32)
    if cols: v *= np.repeat(np.exp2(rng.integers(-cols, cols + 1, shape[:-2] + (1, shape[-1] // 4))) * (rng.random(shape[:-2] + (1, shape[-1] // 4)) > 0.0625), 4, axis=-1).astype(np.float32)
    return mx_ref.flush(v.astype(BF))
C, J = 288, 128
STEP = [1, 2, 4]
def big(v):
    v = v.astype(np.float32)
    v[np.abs(v) < np.float32(2.0 ** -12)] = 0
    return v.astype(BF)
def numbers_of(rng):
    return {"x": big(f(rng, N, 128, 4 * C)), "u": np.array(f(rng, N, 128, 512)), "v": np.array(f(rng, N, 128, 512))}
def maps_of(rng):
    return rng.permuted(np.tile(np.arange(C), (N, 8, 1)), axis=2)
def arrivals(rng, m, right=0.75):
    return np.where(rng.random((N, 8, 4, C)) < right, m[:, :, None], rng.integers(0, C, (N, 8, 4, C)))
def lists(m, a):
    return {"mp": np.stack([gtable(m[r]) for r in range(N)]), "ar": np.stack([gtable(a[r].reshape(8, 4 * C)) for r in range(N)])}
def layers(rng):
    return big(f(rng, N, 128, 2048)).reshape(N, 128, 4, 128, 4)
def weights(rng, w):
    c, s = packed(np.ascontiguousarray(w).reshape(N, 128, 2048), rng)
    return {"wc": c, "ws": s}
def setup_inputs(rng):
    m = maps_of(rng)
    return {**numbers_of(rng), **lists(m, arrivals(rng, m)), **weights(rng, layers(rng))}
def setup_inputs_ties(rng):
    d = numbers_of(rng)
    o = rng.permutation(N)
    x = d["x"].reshape(N, 128, C, 4)
    x[:, :8, :, :2] = rng.integers(0, 3, (N, 8, C, 2)).astype(np.float32).astype(BF)
    x[:, 8:16, :, :2] = 1
    x[o[0], :16, :, :2] = 0
    u = d["u"].reshape(N, 128, 128, 4)
    u[:, :, ::16] = 0
    u[:, :, 1::16] = 0
    w = layers(rng)
    for e in range(2):
        for p in range(16):
            w[:, :, e, p] = 0
            w[:, p, e, p, e] = 32
        for g in range(8):
            for h in range(0, 16, 8):
                w[:, :, e, 16 * g + h] = 0
                w[:, g + h, e, 16 * g + h, e] = 32
                u[:, 16 * g + h, 16 * g + e, e] = 1.0 if h == 0 else -1.0
    m = maps_of(rng)
    for r in range(N): m[r, 1:] = rng.permutation(C)[:8][rng.integers(0, 8, (7, C))]
    one = int(o[1])
    goal = int(m[one, 1, 0])
    m[one, 1] = goal
    right = np.array([1.0, 0.75] + [0.25] * 6)[:, None, None]
    a = arrivals(rng, m, right)
    a[one, 1] = m[one, 1]
    a[one, 2, :, goal] = (m[one, 2, goal] + 1 + np.arange(4)) % C
    x[one, 2, m[one, 0, :J], :2] = 0
    x[one, 2, m[one, 0, 0], :2] = 2
    return {"x": x.reshape(N, 128, 4 * C), "u": u.reshape(N, 128, 512), "v": d["v"], **lists(m, a), **weights(rng, w)}
def setup_inputs_near(rng):
    d = numbers_of(rng)
    x = d["x"].reshape(N, 128, C, 4)
    x.reshape(N, 8, 16, C, 4)[:, :, 8:] = 1
    u = d["u"].reshape(N, 128, 128, 4)
    u[:, :, ::16] = 0
    u[:, :, 1::16] = 0
    o = rng.permutation(N) % 4
    m = maps_of(rng)
    for r in range(N):
        t = np.array([[9.0, 8.0], [11.0, 10.0], [10.0, 9.0]])[rng.integers(0, 3, (8, C, 2))].reshape(8, C, 4) * 0.125
        far = m[r, 0, rng.permutation(J)[:12]]
        if o[r] % 2 == 0: t = t * 2.0 ** -12
        if o[r] < 2:
            t[:, far[:8]] *= 2.0 ** 25 if o[r] == 0 else 2.0 ** 13
            x[r, 15] = 0
            x[r, 15, far[8:], 0] = 1
        x[r, :8] = t.astype(np.float32).astype(BF)
        k = 2.0 ** -30 if o[r] % 2 == 0 else 1.0
        for h in range(0, 128, 16):
            for b in range(2):
                u[r, h + 8 + 2 * b, h + b, 0] = 1.125 * k
                u[r, h + 9 + 2 * b, h + b, 0] = -1.25 * k
                if o[r] < 2: u[r, 16, h + b, 0] = 2.0 ** 30
    w = layers(rng)
    w.reshape(N, 128, 4, 8, 16, 4)[:, :, :, :, 8:] = 0
    w[:, :, :, :8] = 0
    w[:, :, 0, 16] = 0
    w[:, 15, 0, 16, 0] = 32
    for g in range(8):
        for i in range(4):
            w[:, g, i, g, i] = 32
            w[:, g, 0, 16 * g + 8 + i, i] = 2.0 ** -13
    return {"x": x.reshape(N, 128, 4 * C), "u": u.reshape(N, 128, 512), "v": d["v"], **lists(m, arrivals(rng, m)), **weights(rng, w)}
def setup_inputs_ends(rng):
    o = rng.permutation(N) % 4
    x = rng.choice([-1.0, 1.0], (N, 128, 4 * C))
    u = rng.choice([-1.0, 1.0], (N, 128, 128, 4))
    v = rng.choice([-1.0, 1.0], (N, 128, 512))
    m, a = np.zeros((N, 8, C), int), np.full((N, 8, 4, C), C - 1)
    for r in range(N):
        if o[r] == 0:
            x[r] = 1.0
            u[r] = u[r, :1, :, :1].copy()
        if o[r] % 2 == 0: m[r] = C - 1
        if o[r] == 2: a[r, :, ::3] = 0
        if o[r] == 3:
            x[r] = -1.0
            m[r] = np.arange(C)
            a[r] = np.arange(C)[::-1]
        x[r] *= 2.0 ** -12 if o[r] == 2 else 2.0 ** 14
        u[r] *= 2.0 ** -30 if o[r] == 2 else 2.0 ** 30
        v[r] *= 2.0 ** -30 if o[r] == 2 else 2.0 ** 30
    w = np.full((N, 128, 4, 128, 4), 4.0)
    w[:, :, :3, :, :2] = 8.0
    w[:, :, :3, :, 2:] = 0.0
    w[:, :, 3] *= rng.choice([-1.0, 1.0], (N, 128, 128, 4))
    return {"x": x.astype(BF), "u": u.reshape(N, 128, 512).astype(BF), "v": v.astype(BF), **lists(m, a), **weights(rng, w.astype(BF))}
def setup_inputs_blocks(rng):
    d = numbers_of(rng)
    s = (1.0 + (2 * rng.integers(0, 64, (N, 16, 8, C, 4)) + 1) * 2.0 ** -7) * np.exp2(-rng.integers(8, 15, (N, 16, 8, C, 4)).astype(np.float64))
    top = np.arange(32).reshape(8, 1, 4) == rng.integers(0, 32, (N, 16, C))[:, :, None, :, None]
    x = np.where(top, 1.96875, s) * rng.choice([-1.0, 1.0], (N, 16, 8, C, 4)) * np.exp2(rng.integers(2, 8, (N, 16, 1, C, 1)).astype(np.float64))
    m = maps_of(rng)
    return {"x": x.reshape(N, 128, 4 * C).astype(np.float32).astype(BF), "u": d["u"], "v": d["v"], **lists(m, arrivals(rng, m)), **weights(rng, layers(rng))}
def setup_inputs_spread(rng):
    d = setup_inputs(rng)
    d["x"] = big(wide(rng, N, 128, 4 * C, cols=4).astype(np.float32) * np.float32(2.0 ** -5))
    return d
def check_inputs(d):
    b = []
    for k, lo, hi in (("x", 2.0 ** -12, 2.0 ** 14), ("u", 2.0 ** -30, 2.0 ** 30), ("v", 2.0 ** -30, 2.0 ** 30)):
        a = np.abs(d[k].astype(np.float32))
        if not (np.isfinite(a).all() and ((a == 0) | (a >= lo) & (a <= hi)).all()): b.append("a value of " + k)
    for k in ("mp", "ar"):
        if not ((d[k] >= 0) & (d[k] < C)).all(): b.append("an entry of " + k)
    none, least, most = [emit(mx_ref.quantize(np.full((128, 16), k, np.float32).astype(BF)))[1][0, 0] for k in (0.0, 2.0 ** -30, 2.0 ** 30)]
    for r in range(N):
        if ((d["wc"][r] == 0x7F) | (d["wc"][r] == 0xFF)).any(): b.append("wc: a code that is no number")
        s = mx_ref.live(d["ws"][r])
        if ((s != none) & ((s < least) | (s > most))).any(): b.append("ws: a scale out of range")
        else:
            a = np.abs(decode(pk(d["wc"][r], d["ws"][r]))).reshape(128, 512, 4)
            if (np.sum(a, axis=(0, 2), dtype=np.float64) > 2048).any(): b.append("a column of W")
    return b
def chains(m):
    e = [np.arange(J)]
    for g in range(8): e.append(m[g, e[g]])
    return np.stack(e[:8]), np.stack(e[1:])
def reference(x, u, v, mp, ar, wc, ws):
    qu = [mx_ref.quantize(u[r]) for r in range(N)]
    lay = [pk(wc[r], ws[r]) for r in range(N)]
    now = [x[r] for r in range(N)]
    maps = np.stack([gentries(mp[r]) for r in range(N)])
    cand = np.stack([gentries(ar[r]).reshape(8, 4, C) for r in range(N)])
    grp = np.arange(8)
    for h in STEP:
        for r in range(N):
            donor = (r + h) % N
            old = decode(mx_ref.quantize(now[r])).astype(BF)
            e, l = chains(maps[r])
            m = mx_ref.quantize(gcols(old, l))
            q = mx_ref.quantize(tile([np.maximum(mx_ref.matmul(pick(lay[donor], np.arange(128 * b, 128 * b + 128)), m), np.float32(0.0)) * np.float32(0.03125) for b in range(4)]))
            s = mx_ref.matmul(qu[r], q)
            a = cand[r][grp[:, None], 2 * (s[::16] > 0) + (s[1::16] > 0), e]
            wrong = a != l
            first = np.argmax(wrong, axis=0)
            for j in range(J - 1, -1, -1):
                g = first[j]
                if wrong[g, j]: maps[r, g, e[g, j]] = a[g, j]
            l = chains(maps[r])[1]
            n = np.tile(J + np.arange(C), (8, 1))
            for j in range(J - 1, -1, -1): n[grp, l[:, j]] = j
            other = gcols(np.concatenate([decode(q).astype(BF), old], axis=1), n)
            now[r] = ((old.astype(np.float32) + other.astype(np.float32)) * np.float32(0.5)).astype(BF)
    y, fo = np.zeros((N, 128, C), np.float32), np.zeros((N, 8, C), np.float32)
    oc, osc = np.zeros((N, 128, 4 * C), np.uint8), np.zeros((N, 16, C), np.uint8)
    for r in range(N):
        q = mx_ref.quantize(now[r])
        y[r] = mx_ref.matmul(mx_ref.quantize(v[r]), q)
        fo[r] = maps[r]
        oc[r], osc[r] = emit(q)
    return {"y": y, "fo": fo, "oc": oc, "osc": osc}

@@ -1,0 +1,588 @@
+from concourse.mybir import dt, AluOpType as OP, AxisListType, ActivationFunctionType as AF
+
+N, C, J = 8, 288, 128
+STEP = [1, 2, 4]
+MAGIC = 12582912.0
+NONE = 2304
+PARK = 2320
+TAB = PARK + J
+XPAD = 4 * (C + J)
+
+F32, BF, I32, U16, Q8, U8 = "float32", "bfloat16", "int32", "uint16", "float8_e4m3fn_x4", "uint8"
+_S = {
+    "ramp": ([128, 288], F32), "ones": ([128, 128], BF), "ident": ([128, 128], BF), "et": ([128, 2048], BF), "et1": ([128, 2048], BF),
+    "pI": ([128, 1], I32), "cI": ([128, 16], I32), "cF": ([128, 16], F32), "i42": ([128, 4], F32), "e16": ([128, 128], F32),
+    "mask16": ([128, 128], F32), "seg": ([128, 128], F32), "i8": ([128, 8], F32), "upI": ([128, 8], F32), "cG": ([128, 32], F32),
+    "k288": ([128, 32], F32), "K2": ([128, 64], F32), "lrI": ([128, 2], F32), "pl": ([128, 4], F32), "jfr": ([128, 128], F32),
+    "jrl": ([128, 8], F32), "jf": ([128, 8], F32), "park": ([128, 8], F32), "park2": ([128, 8], F32), "jcp": ([128, 1], F32),
+    "mg": ([128, 32], F32), "nmg": ([128, 32], F32), "ah": ([128, 4], F32), "al": ([128, 4], F32), "xh": ([128, 4], F32),
+    "xl": ([128, 4], F32), "ls": ([128, 4], F32), "ls2": ([128, 4], F32), "s2": ([128, 4], F32), "lrf": ([128, 2], F32), "upf": ([128, 8], F32),
+    "dupu": ([128, 4], U16), "selu": ([128, 4], U16), "upu": ([128, 8], U16), "lru": ([128, 2], U16), "eru": ([128, 2], U16),
+    "offa": ([128, 32], U16), "mpI": ([128, 18], I32), "mpF": ([128, 32], F32), "U0": ([128, 32], F32), "U1": ([128, 64], F32),
+    "U2": ([128, 64], F32), "U3": ([128, 36], F32), "AL": ([128, 144], F32), "ALu": ([128, 144], U16), "tab": ([128, TAB], F32),
+    "arI": ([128, 72], I32), "aru": ([128, 72], U16), "cand": ([128, 1152], F32),
+    "xin": ([128, 1152], BF), "uin": ([128, 512], BF), "vin": ([128, 512], BF),
+    "G64": ([128, 64], F32), "TR": ([128, 512], F32), "AQ": ([128, 72], F32), "Lu": ([128, 16], U16), "Lf": ([128, 16], F32),
+    "Fh": ([128, 1152], BF), "XB": ([128, XPAD], BF), "MT": ([128, 512], BF), "ZT": ([128, 512], BF), "ZD": ([128, 512], BF),
+    "HT": ([128, 512], BF), "Hh": ([128, 512], BF), "oc1": ([128, 32], F32), "ocu": ([128, 32], U16), "AN": ([128, 512], F32),
+    "AT": ([128, 512], F32), "AC": ([128, 32], F32), "wr": ([128, 32], F32), "e1": ([128, 32], F32), "a5": ([128, 32], F32),
+    "r1": ([128, 32], F32), "R": ([128, 32], F32), "G2": ([128, 64], F32), "Q2": ([128, 64], F32), "q3": ([128, 32], F32),
+    "q4": ([128, 32], F32), "r": ([128, 1], F32), "km": ([128, 1], F32), "X64": ([128, 64], F32), "XT": ([128, 64], F32),
+    "FC": ([128, 128], F32), "FA": ([128, 128], F32), "aD": ([128, 128], F32), "mk": ([128, 128], F32), "scn": ([128, 128], F32),
+    "nt": ([128, 8], F32), "krl": ([128, 8], F32), "DD": ([128, 1024], F32), "mm": ([128, 8], F32), "lo": ([128, 8], F32),
+    "e2": ([128, 8], F32), "o2": ([128, 8], F32), "ou": ([128, 8], U16), "cb": ([128, 128], F32), "nt2": ([128, 16], F32),
+    "m2": ([128, 8], F32), "jm": ([128, 8], U16), "lo2": ([128, 8], F32), "e3": ([128, 8], F32), "o3": ([128, 8], F32),
+    "XLu": ([128, 32], U16), "ysb": ([128, 288], F32),
+}
+for _n, _w in (("eh", 512), ("e1", 512), ("u", 128), ("up", 128), ("v", 128), ("w", 512), ("wd", 512), ("x", 288), ("z", 128), ("m1", 128), ("m2", 128),
+               ("m3", 128), ("h1", 128), ("h2", 128), ("h3", 128), ("lm1", 128), ("lm2", 128), ("lh1", 128), ("lh2", 128),
+               ("ym1", 128), ("ym2", 128), ("yh1", 128), ("yh2", 128), ("yw", 256)):
+    _S["q_" + _n] = ([128, _w], Q8)
+    _S["s_" + _n] = ([128, _w], U8)
+AT_ = {}
+_PACK = {F32: ("fpack", [0]), U16: ("upack", [0])}
+for _n, (_sh, _d) in list(_S.items()):
+    if _d in _PACK and _sh[1] <= 128 and _n not in ("U0", "AQ"):
+        _b, _o = _PACK[_d]
+        AT_[_n] = (_b, _o[0], _sh[1])
+        _o[0] += (_sh[1] + 7) // 8 * 8
+        del _S[_n]
+for _b, _d in (("fpack", F32), ("upack", U16)):
+    _S[_b] = ([128, _PACK[_d][1][0]], _d)
+SCRATCH = {k: ("sbuf", a, b) for k, (a, b) in _S.items()}
+for _i in range(8):
+    SCRATCH["p%d" % _i] = ("psum", [128, 512], F32)
+NDMA = 20
+SEMAPHORES = ["cv", "ca", "cp", "cg", "sent", "rw", "aw"] + ["d%d" % i for i in range(NDMA)] + [a + b for a in ("r", "a") for b in ("m1", "m2", "h1", "h2")]
+PSKEYS = ["p%d" % i for i in range(8)]
+
+
+def relays(topo, src, dst, same):
+    return [c for c in topo.cores_of(src) if c != src and (topo.die(c) == topo.die(src)) == same and topo.may_write(c, dst)][:2]
+
+
+def pieces(T, tag, src, dst, qs):
+    return T["q_" + tag][:, qs[0]:qs[1]].bitcast(dt.uint8), T["s_" + tag][:, qs[0]:qs[1]]
+
+
+def edges(T, t):
+    for r in range(N):
+        yield "m%d" % t, T.cores[r], T.cores[(r + STEP[t - 1]) % N]
+        yield "h%d" % t, T.cores[(r + STEP[t - 1]) % N], T.cores[r]
+
+
+def hand_on(g, core, T, topo):
+    sent = 0
+    def put(dst, out, inp, sem):
+        rid, pid = topo.addr(dst, core)
+        g.remote_dma(out, inp, T.sem[sem], T.sem["sent"], pid, rid, topo.mask(core, dst))
+        return len(topo.engines(core, dst))
+    todo = [("w", T.cores[(r + STEP[2]) % N], T.cores[r]) for r in range(N)]
+    for t in (1, 2):
+        e = list(edges(T, t))
+        todo += [a for a in e if a[0][0] == "m"] + [a for a in e if a[0][0] == "h"]
+    for tag, src, dst in todo:
+        if core not in topo.cores_of(src) or topo.may_write(src, dst):
+            continue
+        rel = relays(topo, src, dst, tag != "w")
+        if core not in rel:
+            continue
+        k = rel.index(core)
+        n = len(topo.engines(src, core))
+        if tag == "w":
+            g.wait_ge(T.sem["rw"], 2 * n)
+            q, s = pieces(T, "yw", src, dst, (0, 256))
+            q2, s2 = pieces(T, "wd", src, dst, (256 * k, 256 * k + 256))
+            sent += put(dst, q2, q, "aw")
+            sent += put(dst, s2, s, "aw")
+        else:
+            g.wait_ge(T.sem["r" + tag], n)
+            a, b = pieces(T, "y" + tag, src, dst, (0, 128))[k], pieces(T, "l" + tag, src, dst, (0, 128))[k]
+            sent += put(dst, b, a, "a" + tag)
+    if sent:
+        g.wait_ge(T.sem["sent"], sent)
+
+
+def rank_program(g, core, T, topo):
+    rank = T.rank_of(core)
+    if rank is None:
+        hand_on(g, core, T, topo)
+        return
+    eng = {"v": g.vector, "a": g.scalar, "p": g.tensor, "g": g, "s": g.sync}
+    csem = {"v": "cv", "a": "ca", "p": "cp", "g": "cg"}
+    cnt = {"cv": 0, "ca": 0, "cp": 0, "cg": 0, "sent": 0}
+    clock = {q: {} for q in eng}
+    lastw, readers = {}, {}
+    ndma = [0]
+
+    def waits(q, rd, wr):
+        need = []
+        for k in rd:
+            if k in lastw:
+                need.append(lastw[k])
+        for k in wr:
+            toks = ([lastw[k]] if k in lastw else []) + readers.get(k, [])
+            need += [t for t in toks if t[2] != q]
+        for sem, lev, pq, snap in sorted(need, key=lambda t: -t[1]):
+            if clock[q].get(sem, 0) >= lev:
+                continue
+            eng[q].wait_ge(T.sem[sem], lev)
+            for a, b in snap.items():
+                if clock[q].get(a, 0) < b:
+                    clock[q][a] = b
+
+    def note(tok, rd, wr):
+        for k in rd:
+            readers.setdefault(k, []).append(tok)
+        for k in wr:
+            lastw[k] = tok
+            readers[k] = []
+
+    def op(q, rd, wr, fn):
+        ps = [k for k in rd if k in PSKEYS]
+        rd2 = [k for k in rd if k not in PSKEYS]
+        wr2 = list(wr) + ps
+        waits(q, rd2, wr2)
+        sem = csem[q]
+        cnt[sem] += 1
+        fn(eng[q]).then_inc(T.sem[sem], 1)
+        snap = dict(clock[q])
+        snap[sem] = cnt[sem]
+        note((sem, cnt[sem], q, snap), rd2, wr2)
+
+    def dma(q, out, inp):
+        waits(q, inp[1], out[1])
+        sem = "d%d" % ndma[0]
+        ndma[0] += 1
+        cnt[sem] = 16
+        eng[q].dma_start(out[0], inp[0]).then_inc(T.sem[sem], 16)
+        snap = dict(clock[q])
+        snap[sem] = 16
+        note((sem, 16, "dma", snap), inp[1], out[1])
+
+    def arrive(tag, n, keys):
+        cnt[tag] = n
+        note((tag, n, "ext", {tag: n}), [], keys)
+
+    def B(name, a=None, b=None, st=None, p0=0, p1=128, key=None):
+        k = [name] if key is None else ([key] if isinstance(key, str) else list(key))
+        buf, o, w = AT_[name] if name in AT_ else (name, 0, T[name].shape[1])
+        lo, hi = o + (a or 0), o + (w if b is None else b)
+        return T[buf][p0:p1, lo:hi:st] if st else T[buf][p0:p1, lo:hi], k
+
+    def IND(win, off):
+        return win[0].indirect(off[0]), win[1] + off[1]
+
+    def X(o):
+        return (o[0], o[1]) if isinstance(o, tuple) else (o, [])
+
+    def vcopy(o, i):
+        op("v", i[1], o[1], lambda e: e.tensor_copy(o[0], i[0]))
+
+    def acopy(o, i, scale=1.0, func=AF.Copy):
+        op("a", i[1], o[1], lambda e: e.activation(o[0], i[0], func, scale=scale))
+
+    def copy(q, o, i):
+        (vcopy if q == "v" else acopy)(o, i)
+
+    def vts(o, i, s1, op0, s2=None, op1=None):
+        a, b = X(s1), X(s2)
+        if op1 is None:
+            op("v", i[1] + a[1], o[1], lambda e: e.tensor_scalar(o[0], i[0], a[0], None, op0))
+        else:
+            op("v", i[1] + a[1] + b[1], o[1], lambda e: e.tensor_scalar(o[0], i[0], a[0], b[0], op0, op1))
+
+    def vtt(o, i, j, o_):
+        op("v", i[1] + j[1], o[1], lambda e: e.tensor_tensor(o[0], i[0], j[0], o_))
+
+    def vmem(o, c):
+        op("v", [], o[1], lambda e: e.memset(o[0], c))
+
+    def vtr(o, i):
+        op("v", i[1], o[1], lambda e: e.transpose(o[0], i[0]))
+
+    def quant(tag, i, a=0, b=None):
+        q, s = B("q_" + tag), B("s_" + tag)
+        op("v", i[1], q[1] + s[1], lambda e: e.quantize_mx(q[0], s[0], i[0]))
+
+    def mmx(o, l, l0, r, n):
+        lq, lsc, rq, rsc = B("q_" + l, l0, l0 + 128), B("s_" + l, l0, l0 + 128), B("q_" + r, 0, n), B("s_" + r, 0, n)
+        op("p", lq[1] + lsc[1] + rq[1] + rsc[1], [o], lambda e: e.matmul_mx(T[o][:, 0:n], lq[0], lsc[0], rq[0], rsc[0], True, True))
+
+    def iota(o, pattern, base=0, cm=0, f=True):
+        if f:
+            op("g", [], o[1], lambda e: e.iota(o[0], pattern, base, cm, allow_small_or_imprecise_dtypes=True))
+        else:
+            op("g", [], o[1], lambda e: e.iota(o[0], pattern, base, cm))
+
+    def put(dst, out, inp, sem):
+        rid, pid = topo.addr(dst, core)
+        g.remote_dma(out, inp, T.sem[sem], T.sem["sent"], pid, rid, topo.mask(core, dst))
+        cnt["sent"] += len(topo.engines(core, dst))
+
+    def send(tag, dst):
+        waits("g", ["q_" + tag, "s_" + tag], [])
+        src = pieces(T, tag, core, dst, (0, 128))
+        rel = None if topo.may_write(core, dst) else relays(topo, core, dst, True)
+        for k in range(2):
+            if rel is None:
+                put(dst, pieces(T, "l" + tag, core, dst, (0, 128))[k], src[k], "a" + tag)
+            else:
+                put(rel[k], pieces(T, "y" + tag, core, dst, (0, 128))[k], src[k], "r" + tag)
+
+    def arrival_count(src, dst, same, calls):
+        if topo.may_write(src, dst):
+            return calls * len(topo.engines(src, dst))
+        return calls * len(topo.engines(relays(topo, src, dst, same)[0], dst))
+
+    dma("s", B("mpI"), (T.mp[:], []))
+    dma("s", B("xin"), (T.x[:], []))
+    dma("a", B("arI"), (T.ar[:], []))
+    dma("a", B("uin"), (T.u[:], []))
+    dma("s", (T["q_w"][:].bitcast(dt.uint8), ["q_w"]), (T.wc[:], []))
+    dma("s", B("s_w"), (T.ws[:], []))
+    dma("s", B("vin"), (T.v[:], []))
+
+    vmem(B("ones"), 1.0)
+    vmem(B("mpF"), 0.0)
+    iota(B("pI"), [[0, 1]], 0, 1, False)
+    iota(B("i42"), [[16, 2], [0, 2]])
+    iota(B("ramp"), [[1, 288]])
+    idn = B("ident")
+    on = B("ones")
+    op("g", on[1], idn[1], lambda e: e.affine_select(idn[0], on[0], [[-1, 128]], OP.is_equal, 0.0, 0, 1))
+    iota(B("upI"), [[1, 4], [64, 2]])
+    iota(B("lrI"), [[8, 2]], 2)
+    iota(B("pl"), [[-2, 2], [0, 2]], 2)
+    iota(B("i8"), [[16, 8]])
+    iota(B("k288"), [[0, 4], [288, 4], [0, 2]])
+    iota(B("cG"), [[576, 4], [0, 4], [288, 2]], -NONE)
+    iota(B("K2", 0, 32), [[0, 4], [1, 2], [0, 4]])
+    iota(B("K2", 32, 64), [[0, 8], [1, 2], [0, 2]])
+    iota(B("e16"), [[0, 8], [1, 16]])
+
+    def ci(c, sh, an):
+        o, i = B("cI", c, c + 1), B("pI")
+        if sh and an:
+            vts(o, i, sh, OP.logical_shift_right, an, OP.bitwise_and)
+        elif sh:
+            vts(o, i, sh, OP.logical_shift_right)
+        else:
+            vts(o, i, an, OP.bitwise_and)
+
+    def cf(c):
+        return B("cF", c, c + 1)
+    for c, (sh, an) in enumerate(((0, 15), (0, 111), (3, 1), (0, 1), (4, 1), (2, 1), (1, 1), (6, 1), (5, 1), (4, 0))):
+        ci(c, sh, an)
+    vcopy(B("cF", 10, 11), B("pI"))
+    vcopy(B("cF", 0, 10), B("cI", 0, 10))
+    vts(B("dupu"), B("i42"), cf(0), OP.add)
+    vts(B("offa", 0, 4), B("i42"), cf(1), OP.add)
+    vts(B("AQ", 0, 2, key="AQa"), B("i42", 0, 4, 2), cf(1), OP.add)
+    vmem(B("et"), 0.0)
+    for b in range(4):
+        acopy(B("et", 512 * b + b, 512 * b + 512, 4), B("ident"), 0.5)
+
+    vcopy(B("mpF", 0, 18), B("mpI"))
+    vtr(B("U0"), B("mpF"))
+    vcopy(B("U1"), IND(B("U0"), B("dupu")))
+    vtr(B("U2"), B("U1"))
+    vcopy(B("U3", 0, 18, key="U3a"), B("U2", 0, 18))
+    acopy(B("U3", 18, 36, key="U3b"), B("U2", 32, 50))
+
+    def spread(dst, w, src, s0, skeys, engines):
+        n = 0
+        for a in range(4):
+            for d in (0, 1):
+                e = a ^ d
+                copy(engines[n % len(engines)], B(dst, w * a, w * a + w, p0=32 * e, p1=32 * e + 32, key="%s.%d.%d" % (dst, a, e)),
+                     B(src, s0, s0 + w, p0=32 * a, p1=32 * a + 32, key=skeys))
+                n += 1
+        for h in (0, 1):
+            ks = ["%s.%d.%d" % (dst, a, e) for a in (2 * h, 2 * h + 1) for e in (2 * h, 2 * h + 1)]
+            copy(engines[(n + h) % len(engines)], B(dst, 2 * w * h, 2 * w * h + 2 * w, p0=64 - 64 * h, p1=128 - 64 * h, key="%s.h%d" % (dst, h)),
+                 B(dst, 2 * w * h, 2 * w * h + 2 * w, p0=64 * h, p1=64 * h + 64, key=ks))
+        return ["%s.%d.%d" % (dst, a, a ^ d) for a in range(4) for d in (0, 1)] + [dst + ".h0", dst + ".h1"]
+
+    alk = spread("AL", 36, "U3", 0, ("U3a", "U3b"), "va")
+    vcopy(B("ALu"), B("AL", key=alk))
+    for m in range(8):
+        copy("v" if m in (0, 3, 6) else "a", B("tab", C * m, C * m + C, key="t%d" % m), IND(B("ramp"), B("ALu", 18 * m, 18 * m + 18)))
+    tabk = ["t%d" % m for m in range(8)]
+
+    vcopy(B("ah", 0, 1), cf(5))
+    vcopy(B("ah", 1, 2), cf(5))
+    vmem(B("ah", 2, 3), 0.0)
+    vmem(B("ah", 3, 4), 1.0)
+    vcopy(B("al", 0, 1), cf(6))
+    vcopy(B("al", 1, 2), cf(6))
+    vcopy(B("al", 2, 3), cf(2))
+    vcopy(B("al", 3, 4), cf(2))
+    vts(B("ah"), B("ah"), cf(7), OP.subtract)
+    vts(B("al"), B("al"), cf(8), OP.subtract)
+    vtt(B("xh"), B("ah"), B("ah"), OP.mult)
+    vtt(B("xl"), B("al"), B("al"), OP.mult)
+    vts(B("s2", 0, 1, key="s2a"), cf(9), 2.0, OP.mult, cf(3), OP.add)
+    vts(B("ls"), B("xh"), 36.0, OP.mult, B("s2", 0, 1, key="s2a"), OP.add)
+    vts(B("xl"), B("xl"), 18.0, OP.mult)
+    vtt(B("ls"), B("ls"), B("pl"), OP.add)
+    vtt(B("ls2"), B("ls"), B("xl"), OP.add)
+    vcopy(B("selu"), B("ls2"))
+
+    def chain(first=False):
+        for m in range(8):
+            t = B("TR", 64 * m, 64 * m + 64, key="TR%d" % m)
+            off = B("offa", 4 * m, 4 * m + 4, key="offa" if m == 0 else "of%d" % m)
+            vcopy(B("G64"), IND(B("tab", C * m, C * m + C, key="t%d" % m), off))
+            vtr(t, B("G64"))
+            two = B("TR", 64 * m + 31, 64 * m + 33, key="TR%d" % m)
+            if m < 7:
+                vcopy(B("offa", 4 * m + 4, 4 * m + 8, key="of%d" % (m + 1)), B("TR", 64 * m + 30, 64 * m + 34, key="TR%d" % m))
+                acopy(B("AQ", 2 * m + 2, 2 * m + 4, key="AQc"), two)
+            else:
+                vcopy(B("AQ", 16, 18, key="AQb"), two)
+        for a in range(4):
+            copy("va"[a % 2], B("AQ", 18, 36, p0=32 * a, p1=32 * a + 32, key="AQ1.%d" % a),
+                 B("AQ", 0, 18, p0=32 * (a ^ 1), p1=32 * (a ^ 1) + 32, key=("AQa", "AQb", "AQc")))
+        for h in (0, 1):
+            copy("va"[h], B("AQ", 36, 72, p0=64 * h, p1=64 * h + 64, key="AQ2.%d" % h),
+                 B("AQ", 0, 36, p0=64 - 64 * h, p1=128 - 64 * h, key=("AQa", "AQb", "AQc", "AQ1.%d" % (2 - 2 * h), "AQ1.%d" % (3 - 2 * h))))
+        vcopy(B("Lu"), IND(AQ, B("selu", 0, 1)))
+        vcopy(B("Lf"), IND(AQ, B("selu", 0, 1)))
+
+    AQ = B("AQ", key=("AQa", "AQb", "AQc", "AQ1.0", "AQ1.1", "AQ1.2", "AQ1.3", "AQ2.0", "AQ2.1"))
+    LL = B("Lu", 0, 8)
+
+    def fx():
+        for b in range(4):
+            mmx("p%d" % b, "eh", 128 * b, "x", C)
+        for b in range(4):
+            o, i = B("Fh", C * b, C * b + C, key="Fh%d" % b), B("p%d" % b, 0, C)
+            copy("av"[b % 2], o, i)
+
+    def base():
+        for b in range(4):
+            acopy(B("XB", b, 4 * C, 4), B("p%d" % b, 0, C), 2.0)
+
+    quant("eh", B("et"))
+    quant("x", B("xin"))
+    fx()
+    chain(True)
+    for b in range(4):
+        o, i = B("MT", b, 512, 4, key="MT%d" % b), IND(B("Fh", C * b, C * b + C, key="Fh%d" % b), LL)
+        if b % 2:
+            vts(o, i, 2.0, OP.mult)
+        else:
+            acopy(o, i, 2.0)
+    MT = B("MT", key=("MT0", "MT1", "MT2", "MT3"))
+
+    def send_w():
+        dst = T.cores[(rank - STEP[2]) % N]
+        waits("g", ["q_w", "s_w"], [])
+        if topo.may_write(core, dst):
+            for k in range(2):
+                put(dst, pieces(T, "wd", core, dst, (0, 512))[k], pieces(T, "w", core, dst, (0, 512))[k], "aw")
+        else:
+            rel = relays(topo, core, dst, False)
+            for c in range(2):
+                for k in range(2):
+                    put(rel[c], pieces(T, "yw", core, dst, (0, 256))[k], pieces(T, "w", core, dst, (256 * c, 256 * c + 256))[k], "rw")
+
+    def setup_rest():
+        vcopy(B("aru"), B("arI"))
+        acopy(B("cand"), IND(B("ramp"), B("aru")))
+        vts(B("s2", 1, 2, key="s2b"), cf(2), 2.0, OP.mult, cf(3), OP.add)
+        vts(B("s2", 2, 3, key="s2c"), B("s2", 1, 2, key="s2b"), 2.0, OP.mult, cf(4), OP.add)
+        vts(B("s2", 3, 4, key="s2d"), B("s2", 1, 2, key="s2b"), 16.0, OP.mult)
+        vts(B("upf"), B("upI"), B("s2", 3, 4, key="s2d"), OP.add)
+        vcopy(B("upu"), B("upf"))
+        vts(B("lrf"), B("lrI"), B("s2", 2, 3, key="s2c"), OP.add)
+        vcopy(B("lru"), B("lrf"))
+        vts(B("eru"), B("lrf"), -2.0, OP.add)
+        quant("u", B("uin"))
+        vcopy((T["q_up"][:, 0:128].bitcast(dt.uint32), ["q_up"]), (T["q_u"][:, 0:128].bitcast(dt.uint32).indirect(B("upu")[0]), ["q_u", "upu"]))
+        vcopy(B("s_up"), IND(B("s_u"), B("upu")))
+        vts(B("cG"), B("cG"), 255.5 / 512, OP.subtract)
+        vts(B("jrl"), B("i8"), cf(0), OP.add)
+        vts(B("mask16"), B("e16"), cf(0), OP.is_equal)
+        vts(B("seg"), B("e16"), 0.0, OP.is_gt)
+        vts(B("jf"), B("jrl"), 1.0 / 256, OP.mult)
+        vts(B("park"), B("jrl"), float(PARK), OP.add)
+        vts(B("park2"), B("jrl"), float(C), OP.add)
+        vts(B("jfr"), B("ramp", 0, 128), 1.0 / 256, OP.mult)
+        vts(B("jcp"), cf(10), 1.0 / 256, OP.mult)
+        vmem(B("mg"), MAGIC)
+        vmem(B("nmg"), -MAGIC)
+
+    def setup_late():
+        acopy(B("et1"), B("et"), 2.0)
+        quant("e1", B("et1"))
+        quant("v", B("vin"))
+
+    def asks():
+        vtt(B("oc1"), IND(AQ, B("selu", 2, 4)), B("k288"), OP.add)
+        vcopy(B("ocu"), B("oc1"))
+        acopy(B("AN", 0, 256, key="AN0"), IND(B("cand"), B("ocu", 0, 16)))
+        vcopy(B("AN", 256, 512, key="AN1"), IND(B("cand"), B("ocu", 16, 32)))
+        vtr(B("AT", 256, 512, key="AT1"), B("AN", 256, 512, key="AN1"))
+        vtr(B("AT", 0, 256, key="AT0"), B("AN", 0, 256, key="AN0"))
+        ks = []
+        for a in (2, 3, 0, 1):
+            for b in range(4):
+                k = "AC.%d.%d" % (a, b)
+                ks.append(k)
+                copy("va"[b % 2], B("AC", 8 * b, 8 * b + 8, p0=32 * a, p1=32 * a + 32, key=k),
+                     B("AT", 128 * a, 128 * a + 128, 16, p0=32 * b, p1=32 * b + 32, key="AT%d" % (a // 2)))
+        AC = B("AC", key=ks)
+        vtt(B("wr"), IND(AQ, B("lru")), AC, OP.not_equal)
+        vtt(B("e1"), IND(AQ, B("eru")), B("cG"), OP.add)
+        vts(B("a5"), AC, 1.0 / 512, OP.mult)
+        vtt(B("r1"), B("e1"), B("a5"), OP.add)
+        vtt(B("R"), B("r1"), B("wr"), OP.mult)
+
+    def serve(t):
+        dst = T.cores[(rank - STEP[t - 1]) % N]
+        lay("w", "lm%d" % t, "h%d" % t)
+        send("h%d" % t, dst)
+
+    def lay(w, m, h):
+        for b in range(4):
+            mmx("p%d" % (4 + b), w, 128 * b, m, 128)
+        for b in range(4):
+            o, i = B("HT", b, 512, 4, key="HT%d" % b), B("p%d" % (4 + b), 0, 128)
+            if b % 2:
+                vts(o, i, 0.0, OP.max, 0.03125, OP.mult)
+            else:
+                acopy(o, i, 0.03125, AF.Relu)
+        quant(h, B("HT", key=("HT0", "HT1", "HT2", "HT3")))
+
+    def least(comb, nt, m):
+        for c in range(8):
+            n = 16 * c + 16
+            d, i, bi = B("DD", 128 * c, 128 * c + n, key="DD%d" % c), B(comb[0], 0, n, key=comb[1]), B(nt, c, c + 1)
+            op("a", i[1] + bi[1], d[1], lambda e, d=d, i=i, bi=bi: e.activation(d[0], i[0], AF.Identity, bias=bi[0]))
+        for c in range(8):
+            n = 16 * c + 16
+            d, o = B("DD", 128 * c, 128 * c + n, key="DD%d" % c), B(m, c, c + 1)
+            op("v", d[1], o[1], lambda e, d=d, o=o: e.tensor_reduce(o[0], d[0], AxisListType.X, OP.min, apply_absolute_value=True))
+
+    def scores(h):
+        mmx("p4", h, 0, "up", 128)
+
+    def halves(h):
+        for b in range(4):
+            mmx("p%d" % b, "eh", 128 * b, h, 128)
+        for b in range(4):
+            acopy(B("Hh", 128 * b, 128 * b + 128, key="Hh%d" % b), B("p%d" % b, 0, 128))
+
+    def repair():
+        vts(B("G2"), B("p4", 0, 64), 0.0, OP.is_gt)
+        vtt(B("Q2"), B("G2"), B("K2"), OP.is_equal)
+        vtt(B("q3"), B("Q2", 0, 32), B("Q2", 32, 64), OP.mult)
+        vtt(B("q4"), B("q3"), B("R"), OP.mult)
+        o, i = B("r"), B("q4")
+        op("v", i[1], o[1], lambda e: e.tensor_reduce(o[0], i[0], AxisListType.X, OP.min))
+        vts(B("km"), B("r"), MAGIC, OP.add)
+        vts(B("X64", 0, 32), B("nmg"), B("km"), OP.add, B("jcp"), OP.add)
+        vts(B("X64", 32, 64), B("mg"), B("km"), OP.subtract, B("r"), OP.add)
+        vtr(B("XT"), B("X64"))
+        fck = spread("FC", 32, "XT", 0, "XT", "va")
+        FC = B("FC", key=fck)
+        vtt(B("mk"), FC, B("mask16"), OP.mult)
+        fak = spread("FA", 32, "XT", 32, "XT", "a")
+        sg, mk, sc = B("seg"), B("mk"), B("scn")
+        op("v", sg[1] + mk[1], sc[1], lambda e: e.tensor_tensor_scan(sc[0], sg[0], mk[0], 0.0, OP.mult, OP.add))
+        vtt(B("nt"), B("jf"), B("scn", 15, 128, 16), OP.subtract)
+        vts(B("krl"), B("nt"), -1.0, OP.mult, float(NONE), OP.add)
+        least(("FC", fck), "nt", "mm")
+        FA, aD = B("FA", key=fak), B("aD")
+        op("a", FA[1], aD[1], lambda e: e.activation(aD[0], FA[0], AF.Copy, bias=255.5, scale=512.0))
+        vtt(B("lo"), B("mm"), B("jf"), OP.not_equal)
+        vtt(B("e2"), B("lo"), B("park"), OP.mult)
+        vtt(B("o2"), B("e2"), B("krl"), OP.max)
+        vcopy(B("ou"), B("o2"))
+        op("v", aD[1] + ["ou"] + tabk, tabk, lambda e: e.tensor_copy(T["tab"][:, 0:TAB].indirect(B("ou")[0]), aD[0]))
+
+    def means():
+        vtt(B("cb"), IND(B("ramp"), LL), B("jfr"), OP.add)
+        vts(B("nt2"), B("Lf"), -1.0, OP.mult)
+        for b in range(4):
+            vtt(B("ZT", b, 512, 4), IND(B("Fh", C * b, C * b + C, key="Fh%d" % b), LL), B("Hh", 128 * b, 128 * b + 128, key="Hh%d" % b), OP.add)
+
+    def state():
+        vtt(B("lo2"), B("m2"), B("jf"), OP.not_equal)
+        vtt(B("e3"), B("lo2"), B("park2"), OP.mult)
+        vtt(B("o3"), B("e3"), B("Lf", 0, 8), OP.max)
+        for t in range(4):
+            vts(B("XLu", 8 * t, 8 * t + 8, key="XL%d" % t), B("o3"), 4.0, OP.mult, float(t), OP.add)
+        for t in range(4):
+            op("v", ["ZT", "XL%d" % t, "XB"], ["XB"], lambda e, t=t: e.tensor_copy(T["XB"][:, 0:XPAD].indirect(B("XLu", 8 * t, 8 * t + 8)[0]), T["ZT"][:, t:512:4]))
+        quant("x", B("XB", 0, 4 * C))
+
+    def next_m(tag):
+        quant("z", B("ZT"))
+        for b in range(4):
+            mmx("p%d" % (4 + b), "e1", 128 * b, "z", 128)
+        least(("cb", "cb"), "nt2", "m2")
+        vts(B("jm"), B("m2"), 256.0, OP.mult)
+        for b in range(4):
+            acopy(B("ZD", 128 * b, 128 * b + 128, key="ZD%d" % b), B("p%d" % (4 + b), 0, 128))
+        for b in range(4):
+            copy("av"[b % 2], B("MT", b, 512, 4, key="MT%d" % b), IND(B("ZD", 128 * b, 128 * b + 128, key="ZD%d" % b), B("jm")))
+        quant(tag, MT)
+
+    donor = [T.cores[(rank + s) % N] for s in STEP]
+    asker = [T.cores[(rank - s) % N] for s in STEP]
+    for t in (1, 2):
+        arrive("am%d" % t, arrival_count(asker[t - 1], core, True, 2), ["q_lm%d" % t, "s_lm%d" % t])
+        arrive("ah%d" % t, arrival_count(donor[t - 1], core, True, 2), ["q_lh%d" % t, "s_lh%d" % t])
+    arrive("aw", arrival_count(donor[2], core, False, 2 if topo.may_write(donor[2], core) else 4), ["q_wd", "s_wd"])
+
+    quant("m1", MT)
+    send("m1", donor[0])
+    send_w()
+    setup_rest()
+    asks()
+    serve(1)
+    base()
+    setup_late()
+    scores("lh1")
+    halves("lh1")
+    repair()
+    chain()
+    means()
+    next_m("m2")
+    send("m2", donor[1])
+    asks()
+    serve(2)
+    state()
+    fx()
+    base()
+    scores("lh2")
+    halves("lh2")
+    repair()
+    chain()
+    means()
+    next_m("m3")
+    lay("wd", "m3", "h3")
+    scores("h3")
+    asks()
+    state()
+    fx()
+    base()
+    halves("h3")
+    repair()
+    dma("s", (T.fo[:], []), B("tab", 0, NONE, p0=0, p1=1, key=tabk))
+    chain()
+    means()
+    least(("cb", "cb"), "nt2", "m2")
+    state()
+    mmx("p4", "v", 0, "x", C)
+    acopy(B("ysb"), B("p4", 0, C))
+    dma("s", (T.oc[:], []), (T["q_x"][:, 0:C].bitcast(dt.uint8), ["q_x"]))
+    for k in range(4):
+        dma("s", (T.osc[4 * k:4 * k + 4, :], []), (T["s_x"][32 * k:32 * k + 4, 0:C], ["s_x"]))
+    dma("a", (T.y[:], []), B("ysb"))
+    for sem in cnt:
+        if cnt[sem] and clock["g"].get(sem, 0) < cnt[sem]:
+            g.wait_ge(T.sem[sem], cnt[sem])

@@ -2,7 +2,6 @@ from concourse.mybir import dt, AluOpType as OP, AxisListType, ActivationFunctio
 
 N, C, J = 8, 288, 128
 STEP = [1, 2, 4]
-MAGIC = 12582912.0
 NONE = 2304
 PARK = 2320
 TAB = PARK + J
@@ -10,24 +9,24 @@ XPAD = 4 * (C + J)
 
 F32, BF, I32, U16, Q8, U8 = "float32", "bfloat16", "int32", "uint16", "float8_e4m3fn_x4", "uint8"
 _S = {
-    "ramp": ([128, 288], F32), "ones": ([128, 128], BF), "ident": ([128, 128], BF), "et": ([128, 2048], BF), "et1": ([128, 2048], BF),
+    "ramp": ([128, 288], F32), "half": ([128, 512], BF), "FL": ([128, 256], BF), "et": ([128, 2048], BF), "et1": ([128, 2048], BF),
     "pI": ([128, 1], I32), "cI": ([128, 16], I32), "cF": ([128, 16], F32), "i42": ([128, 4], F32), "e16": ([128, 128], F32),
     "mask16": ([128, 128], F32), "seg": ([128, 128], F32), "i8": ([128, 8], F32), "upI": ([128, 8], F32), "cG": ([128, 32], F32),
     "k288": ([128, 32], F32), "K2": ([128, 64], F32), "lrI": ([128, 2], F32), "pl": ([128, 4], F32), "jfr": ([128, 128], F32),
     "jrl": ([128, 8], F32), "jf": ([128, 8], F32), "park": ([128, 8], F32), "park2": ([128, 8], F32), "jcp": ([128, 1], F32),
-    "mg": ([128, 32], F32), "nmg": ([128, 32], F32), "ah": ([128, 4], F32), "al": ([128, 4], F32), "xh": ([128, 4], F32),
+    "zero": ([128, 32], F32), "ah": ([128, 4], F32), "al": ([128, 4], F32), "xh": ([128, 4], F32),
     "xl": ([128, 4], F32), "ls": ([128, 4], F32), "ls2": ([128, 4], F32), "s2": ([128, 4], F32), "lrf": ([128, 2], F32), "upf": ([128, 8], F32),
     "dupu": ([128, 4], U16), "selu": ([128, 4], U16), "upu": ([128, 8], U16), "lru": ([128, 2], U16), "eru": ([128, 2], U16),
-    "offa": ([128, 32], U16), "mpI": ([128, 18], I32), "mpF": ([128, 32], F32), "U0": ([128, 32], F32), "U1": ([128, 64], F32),
+    "offa": ([128, 4], U16), "mpI": ([128, 18], I32), "mpF": ([128, 32], F32), "U0": ([128, 32], F32), "U1": ([128, 64], F32),
     "U2": ([128, 64], F32), "U3": ([128, 36], F32), "AL": ([128, 144], F32), "ALu": ([128, 144], U16), "tab": ([128, TAB], F32),
     "arI": ([128, 72], I32), "aru": ([128, 72], U16), "cand": ([128, 1152], F32),
     "xin": ([128, 1152], BF), "uin": ([128, 512], BF), "vin": ([128, 512], BF),
-    "G64": ([128, 64], F32), "TR": ([128, 512], F32), "AQ": ([128, 72], F32), "Lu": ([128, 16], U16), "Lf": ([128, 16], F32),
+    "G64": ([128, 64], U16), "TR": ([128, 512], U16), "AQ": ([128, 72], F32), "Lu": ([128, 16], U16), "Lf": ([128, 16], F32),
     "Fh": ([128, 1152], BF), "XB": ([128, XPAD], BF), "MT": ([128, 512], BF), "ZT": ([128, 512], BF), "ZD": ([128, 512], BF),
     "HT": ([128, 512], BF), "Hh": ([128, 512], BF), "oc1": ([128, 32], F32), "ocu": ([128, 32], U16), "AN": ([128, 512], F32),
     "AT": ([128, 512], F32), "AC": ([128, 32], F32), "wr": ([128, 32], F32), "e1": ([128, 32], F32), "a5": ([128, 32], F32),
-    "r1": ([128, 32], F32), "R": ([128, 32], F32), "G2": ([128, 64], F32), "Q2": ([128, 64], F32), "q3": ([128, 32], F32),
-    "q4": ([128, 32], F32), "r": ([128, 1], F32), "km": ([128, 1], F32), "X64": ([128, 64], F32), "XT": ([128, 64], F32),
+    "r1": ([128, 32], F32), "KR": ([128, 64], F32), "G2": ([128, 64], F32), "Q2": ([128, 64], F32), "q3": ([128, 32], F32),
+    "q4": ([128, 64], F32), "rk": ([128, 2], F32), "X64": ([128, 64], F32), "XT": ([128, 64], F32),
     "FC": ([128, 128], F32), "FA": ([128, 128], F32), "aD": ([128, 128], F32), "mk": ([128, 128], F32), "scn": ([128, 128], F32),
     "nt": ([128, 8], F32), "krl": ([128, 8], F32), "DD": ([128, 1024], F32), "mm": ([128, 8], F32), "lo": ([128, 8], F32),
     "e2": ([128, 8], F32), "o2": ([128, 8], F32), "ou": ([128, 8], U16), "cb": ([128, 128], F32), "nt2": ([128, 16], F32),
@@ -39,6 +38,7 @@ for _n, _w in (("eh", 512), ("e1", 512), ("u", 128), ("up", 128), ("v", 128), ("
                ("ym1", 128), ("ym2", 128), ("yh1", 128), ("yh2", 128), ("yw", 256)):
     _S["q_" + _n] = ([128, _w], Q8)
     _S["s_" + _n] = ([128, _w], U8)
+KIND = {k: ("b" if v[1] in (BF, U16) else "f") for k, v in _S.items()}
 AT_ = {}
 _PACK = {F32: ("fpack", [0]), U16: ("upack", [0])}
 for _n, (_sh, _d) in list(_S.items()):
@@ -55,14 +55,15 @@ for _i in range(8):
 NDMA = 20
 SEMAPHORES = ["cv", "ca", "cp", "cg", "sent", "rw", "aw"] + ["d%d" % i for i in range(NDMA)] + [a + b for a in ("r", "a") for b in ("m1", "m2", "h1", "h2")]
 PSKEYS = ["p%d" % i for i in range(8)]
+WAKE = 0.08
 
 
 def relays(topo, src, dst, same):
     return [c for c in topo.cores_of(src) if c != src and (topo.die(c) == topo.die(src)) == same and topo.may_write(c, dst)][:2]
 
 
-def pieces(T, tag, src, dst, qs):
-    return T["q_" + tag][:, qs[0]:qs[1]].bitcast(dt.uint8), T["s_" + tag][:, qs[0]:qs[1]]
+def pieces(T, tag, a, b):
+    return T["q_" + tag][:, a:b].bitcast(dt.uint8), T["s_" + tag][:, a:b]
 
 
 def edges(T, t):
@@ -91,16 +92,80 @@ def hand_on(g, core, T, topo):
         n = len(topo.engines(src, core))
         if tag == "w":
             g.wait_ge(T.sem["rw"], 2 * n)
-            q, s = pieces(T, "yw", src, dst, (0, 256))
-            q2, s2 = pieces(T, "wd", src, dst, (256 * k, 256 * k + 256))
+            q, s = pieces(T, "yw", 0, 256)
+            q2, s2 = pieces(T, "wd", 256 * k, 256 * k + 256)
             sent += put(dst, q2, q, "aw")
             sent += put(dst, s2, s, "aw")
         else:
             g.wait_ge(T.sem["r" + tag], n)
-            a, b = pieces(T, "y" + tag, src, dst, (0, 128))[k], pieces(T, "l" + tag, src, dst, (0, 128))[k]
+            a, b = pieces(T, "y" + tag, 0, 128)[k], pieces(T, "l" + tag, 0, 128)[k]
             sent += put(dst, b, a, "a" + tag)
     if sent:
         g.wait_ge(T.sem["sent"], sent)
+
+
+def depend(nodes):
+    lastw, readers, preds = {}, {}, []
+    for i, nd in enumerate(nodes):
+        rd = [k for k in nd[1] if k not in PSKEYS]
+        wr = list(nd[2]) + [k for k in nd[1] if k in PSKEYS]
+        p = {}
+        for k in nd[1]:
+            if k in lastw:
+                p[lastw[k]] = True
+        for k in wr:
+            for j in ([lastw[k]] if k in lastw else []) + readers.get(k, []):
+                p.setdefault(j, False)
+        p.pop(i, None)
+        preds.append(p)
+        for k in rd:
+            readers.setdefault(k, []).append(i)
+        for k in wr:
+            lastw[k], readers[k] = i, []
+    return preds
+
+
+def schedule(nodes, preds, slack, vp, eps):
+    n = len(nodes)
+    succ = [[] for _ in range(n)]
+    for i, p in enumerate(preds):
+        for j in p:
+            succ[j].append(i)
+    out = [nd[5][1] for nd in nodes]
+    prio = [0.0] * n
+    for i in range(n - 1, -1, -1):
+        prio[i] = min(nodes[i][4].values()) + out[i] + max([prio[k] + (WAKE if preds[k][i] else 0.0) for k in succ[i]] + [0.0])
+    left = [len(p) for p in preds]
+    ready = [i for i in range(n) if not left[i]]
+    qt = {q: 0.0 for q in "gvapsx"}
+    end, where, order = [0.0] * n, [None] * n, []
+
+    def start(i, q):
+        t = 0.0 if q == "x" else qt[q]
+        for j, raw in preds[i].items():
+            if raw or where[j] != q or nodes[j][5][0] != "op":
+                t = max(t, end[j] + out[j] + WAKE)
+        return t
+    while ready:
+        cand = []
+        for i in ready:
+            _, s, q = min((start(i, q) + nodes[i][4][q] + (vp if q == "v" else 0.0), start(i, q), q) for q in nodes[i][0])
+            cand.append((s, q, i))
+        s0, q0, i0 = min(cand)
+        s, q, i = min((c for c in cand if c[1] == q0 and c[0] <= s0 + slack), key=lambda c: (-prio[c[2]], c[2]))
+        fit = [c for c in cand if c[1] == q0 and c[0] + nodes[c[2]][4][q0] <= s + eps and prio[c[2]] < prio[i]]
+        if fit:
+            s, q, i = min(fit, key=lambda c: (-prio[c[2]], c[2]))
+        where[i], end[i] = q, s + nodes[i][4][q]
+        if q != "x":
+            qt[q] = end[i]
+        order.append(i)
+        ready.remove(i)
+        for k in succ[i]:
+            left[k] -= 1
+            if not left[k]:
+                ready.append(k)
+    return max(end), order, where
 
 
 def rank_program(g, core, T, topo):
@@ -108,152 +173,129 @@ def rank_program(g, core, T, topo):
     if rank is None:
         hand_on(g, core, T, topo)
         return
-    eng = {"v": g.vector, "a": g.scalar, "p": g.tensor, "g": g, "s": g.sync}
-    csem = {"v": "cv", "a": "ca", "p": "cp", "g": "cg"}
-    cnt = {"cv": 0, "ca": 0, "cp": 0, "cg": 0, "sent": 0}
-    clock = {q: {} for q in eng}
-    lastw, readers = {}, {}
-    ndma = [0]
+    nodes = []
+    donor = [T.cores[(rank + s) % N] for s in STEP]
+    asker = [T.cores[(rank - s) % N] for s in STEP]
 
-    def waits(q, rd, wr):
-        need = []
-        for k in rd:
-            if k in lastw:
-                need.append(lastw[k])
-        for k in wr:
-            toks = ([lastw[k]] if k in lastw else []) + readers.get(k, [])
-            need += [t for t in toks if t[2] != q]
-        for sem, lev, pq, snap in sorted(need, key=lambda t: -t[1]):
-            if clock[q].get(sem, 0) >= lev:
-                continue
-            eng[q].wait_ge(T.sem[sem], lev)
-            for a, b in snap.items():
-                if clock[q].get(a, 0) < b:
-                    clock[q][a] = b
-
-    def note(tok, rd, wr):
-        for k in rd:
-            readers.setdefault(k, []).append(tok)
-        for k in wr:
-            lastw[k] = tok
-            readers[k] = []
-
-    def op(q, rd, wr, fn):
-        ps = [k for k in rd if k in PSKEYS]
-        rd2 = [k for k in rd if k not in PSKEYS]
-        wr2 = list(wr) + ps
-        waits(q, rd2, wr2)
-        sem = csem[q]
-        cnt[sem] += 1
-        fn(eng[q]).then_inc(T.sem[sem], 1)
-        snap = dict(clock[q])
-        snap[sem] = cnt[sem]
-        note((sem, cnt[sem], q, snap), rd2, wr2)
-
-    def dma(q, out, inp):
-        waits(q, inp[1], out[1])
-        sem = "d%d" % ndma[0]
-        ndma[0] += 1
-        cnt[sem] = 16
-        eng[q].dma_start(out[0], inp[0]).then_inc(T.sem[sem], 16)
-        snap = dict(clock[q])
-        snap[sem] = 16
-        note((sem, 16, "dma", snap), inp[1], out[1])
-
-    def arrive(tag, n, keys):
-        cnt[tag] = n
-        note((tag, n, "ext", {tag: n}), [], keys)
+    def op(qs, rd, wr, fn, cost):
+        nodes.append([qs, list(rd), list(wr), fn, cost if isinstance(cost, dict) else {q: cost for q in qs}, ("op", 0.0)])
 
     def B(name, a=None, b=None, st=None, p0=0, p1=128, key=None):
         k = [name] if key is None else ([key] if isinstance(key, str) else list(key))
         buf, o, w = AT_[name] if name in AT_ else (name, 0, T[name].shape[1])
         lo, hi = o + (a or 0), o + (w if b is None else b)
-        return T[buf][p0:p1, lo:hi:st] if st else T[buf][p0:p1, lo:hi], k
+        kind = "p" if name in PSKEYS else KIND[name]
+        if st:
+            return T[buf][p0:p1, lo:hi:st], k, -(-(hi - lo) // st), kind
+        return T[buf][p0:p1, lo:hi], k, hi - lo, kind
 
     def IND(win, off):
-        return win[0].indirect(off[0]), win[1] + off[1]
+        return win[0].indirect(off[0]), win[1] + off[1], 16 * off[2], "i"
 
     def X(o):
-        return (o[0], o[1]) if isinstance(o, tuple) else (o, [])
+        return o if isinstance(o, tuple) else (o, [], 0, "f")
+
+    def cost(q, o, ins, per=1.0):
+        n = max([o[2]] + [i[2] for i in ins])
+        if any(i[3] == "i" for i in ins):
+            return (0.05 if q == "v" else 0.065) + 0.0015 * n
+        if q == "v" and all(i[3] == "b" for i in list(ins) + [o]) and per == 1.0:
+            per = 0.5
+        return 0.001 * max(64, n * per)
+
+    def flex(qs, o, i, scale=1.0, bias=None, relu=False, after=()):
+        bi = X(bias)
+        def fn(e, q):
+            if q == "a":
+                f = AF.Relu if relu else (AF.Copy if bias is None else AF.Identity)
+                if bias is None and scale == 1.0:
+                    return e.activation(o[0], i[0], f)
+                return e.activation(o[0], i[0], f, scale=scale) if bias is None else e.activation(o[0], i[0], f, bias=bi[0], scale=scale)
+            if relu:
+                return e.tensor_scalar(o[0], i[0], 0.0, scale, OP.max, OP.mult)
+            if bias is None:
+                return e.tensor_copy(o[0], i[0]) if scale == 1.0 else e.tensor_scalar(o[0], i[0], scale, None, OP.mult)
+            return e.tensor_scalar(o[0], i[0], bi[0], None, OP.add)
+        op(qs, i[1] + bi[1] + list(after), o[1], fn, {q: cost(q, o, [i]) for q in qs})
 
     def vcopy(o, i):
-        op("v", i[1], o[1], lambda e: e.tensor_copy(o[0], i[0]))
-
-    def acopy(o, i, scale=1.0, func=AF.Copy):
-        op("a", i[1], o[1], lambda e: e.activation(o[0], i[0], func, scale=scale))
-
-    def copy(q, o, i):
-        (vcopy if q == "v" else acopy)(o, i)
+        op("v", i[1], o[1], lambda e, q: e.tensor_copy(o[0], i[0]), cost("v", o, [i]))
 
     def vts(o, i, s1, op0, s2=None, op1=None):
         a, b = X(s1), X(s2)
         if op1 is None:
-            op("v", i[1] + a[1], o[1], lambda e: e.tensor_scalar(o[0], i[0], a[0], None, op0))
+            op("v", i[1] + a[1], o[1], lambda e, q: e.tensor_scalar(o[0], i[0], a[0], None, op0), cost("v", o, [i]))
         else:
-            op("v", i[1] + a[1] + b[1], o[1], lambda e: e.tensor_scalar(o[0], i[0], a[0], b[0], op0, op1))
+            op("v", i[1] + a[1] + b[1], o[1], lambda e, q: e.tensor_scalar(o[0], i[0], a[0], b[0], op0, op1), cost("v", o, [i]))
 
     def vtt(o, i, j, o_):
-        op("v", i[1] + j[1], o[1], lambda e: e.tensor_tensor(o[0], i[0], j[0], o_))
+        op("v", i[1] + j[1], o[1], lambda e, q: e.tensor_tensor(o[0], i[0], j[0], o_), cost("v", o, [i, j], 1.01 if j[3] == "p" else 2.0))
 
     def vmem(o, c):
-        op("v", [], o[1], lambda e: e.memset(o[0], c))
+        op("v", [], o[1], lambda e, q: e.memset(o[0], c), cost("v", o, []))
 
     def vtr(o, i):
-        op("v", i[1], o[1], lambda e: e.transpose(o[0], i[0]))
+        op("v", i[1], o[1], lambda e, q: e.transpose(o[0], i[0]), cost("v", o, [i]))
 
-    def quant(tag, i, a=0, b=None):
-        q, s = B("q_" + tag), B("s_" + tag)
-        op("v", i[1], q[1] + s[1], lambda e: e.quantize_mx(q[0], s[0], i[0]))
+    def vmin(o, i, mag=False):
+        op("v", i[1], o[1], lambda e, q: e.tensor_reduce(o[0], i[0], AxisListType.X, OP.min, apply_absolute_value=mag), cost("v", o, [i]))
+
+    def quant(tag, i):
+        q_, s_ = T["q_" + tag][:], T["s_" + tag][:]
+        op("v", i[1], ["q_" + tag, "s_" + tag], lambda e, q: e.quantize_mx(q_, s_, i[0]), 0.015 + 0.00027 * i[2])
 
     def mmx(o, l, l0, r, n):
-        lq, lsc, rq, rsc = B("q_" + l, l0, l0 + 128), B("s_" + l, l0, l0 + 128), B("q_" + r, 0, n), B("s_" + r, 0, n)
-        op("p", lq[1] + lsc[1] + rq[1] + rsc[1], [o], lambda e: e.matmul_mx(T[o][:, 0:n], lq[0], lsc[0], rq[0], rsc[0], True, True))
+        lq, lsc, rq, rsc = T["q_" + l][:, l0:l0 + 128], T["s_" + l][:, l0:l0 + 128], T["q_" + r][:, 0:n], T["s_" + r][:, 0:n]
+        op("p", ["q_" + l, "s_" + l, "q_" + r, "s_" + r], [o], lambda e, q: e.matmul_mx(T[o][:, 0:n], lq, lsc, rq, rsc, True, True), 0.001 * (n + 16))
 
     def iota(o, pattern, base=0, cm=0, f=True):
-        if f:
-            op("g", [], o[1], lambda e: e.iota(o[0], pattern, base, cm, allow_small_or_imprecise_dtypes=True))
-        else:
-            op("g", [], o[1], lambda e: e.iota(o[0], pattern, base, cm))
+        def fn(e, q):
+            return e.iota(o[0], pattern, base, cm, allow_small_or_imprecise_dtypes=True) if f else e.iota(o[0], pattern, base, cm)
+        op("g", [], o[1], fn, 0.15 + 0.002 * o[2])
 
-    def put(dst, out, inp, sem):
-        rid, pid = topo.addr(dst, core)
-        g.remote_dma(out, inp, T.sem[sem], T.sem["sent"], pid, rid, topo.mask(core, dst))
-        cnt["sent"] += len(topo.engines(core, dst))
+    def dma(qs, out, inp, size):
+        nodes.append([qs, list(inp[1]), list(out[1]), (out[0], inp[0]), {q: 0.08 for q in qs}, ("dma", 2.0 + size)])
 
     def send(tag, dst):
-        waits("g", ["q_" + tag, "s_" + tag], [])
-        src = pieces(T, tag, core, dst, (0, 128))
-        rel = None if topo.may_write(core, dst) else relays(topo, core, dst, True)
-        for k in range(2):
-            if rel is None:
-                put(dst, pieces(T, "l" + tag, core, dst, (0, 128))[k], src[k], "a" + tag)
-            else:
-                put(rel[k], pieces(T, "y" + tag, core, dst, (0, 128))[k], src[k], "r" + tag)
+        src, rel = pieces(T, tag, 0, 128), None if topo.may_write(core, dst) else relays(topo, core, dst, True)
+        todo = [(dst, pieces(T, "l" + tag, 0, 128)[k], src[k], "a" + tag) if rel is None else
+                (rel[k], pieces(T, "y" + tag, 0, 128)[k], src[k], "r" + tag) for k in range(2)]
+        nodes.append(["g", ["q_" + tag, "s_" + tag], ["out_" + tag], todo, {"g": 1.4}, ("send", 0.0)])
 
-    def arrival_count(src, dst, same, calls):
-        if topo.may_write(src, dst):
-            return calls * len(topo.engines(src, dst))
-        return calls * len(topo.engines(relays(topo, src, dst, same)[0], dst))
+    def send_w():
+        dst = T.cores[(rank - STEP[2]) % N]
+        if topo.may_write(core, dst):
+            todo = [(dst, pieces(T, "wd", 0, 512)[k], pieces(T, "w", 0, 512)[k], "aw") for k in range(2)]
+        else:
+            rel = relays(topo, core, dst, False)
+            todo = [(rel[c], pieces(T, "yw", 0, 256)[k], pieces(T, "w", 256 * c, 256 * c + 256)[k], "rw") for c in range(2) for k in range(2)]
+        nodes.append(["g", ["q_w", "s_w", "out_m1"], ["out_w"], todo, {"g": 2.8}, ("send", 0.0)])
 
-    dma("s", B("mpI"), (T.mp[:], []))
-    dma("s", B("xin"), (T.x[:], []))
-    dma("a", B("arI"), (T.ar[:], []))
-    dma("a", B("uin"), (T.u[:], []))
-    dma("s", (T["q_w"][:].bitcast(dt.uint8), ["q_w"]), (T.wc[:], []))
-    dma("s", B("s_w"), (T.ws[:], []))
-    dma("s", B("vin"), (T.v[:], []))
+    def arrive(tag, src, same, calls, after, lands):
+        straight = topo.may_write(src, core)
+        n = calls * len(topo.engines(src if straight else relays(topo, src, core, same)[0], core))
+        nodes.append(["x", [after], ["q_" + lands, "s_" + lands], n, {"x": 0.0}, ("arr", 3.0 if straight else 6.0, tag)])
 
-    vmem(B("ones"), 1.0)
+    dma("s", B("mpI"), (T.mp[:], []), 0.1)
+    dma("s", B("xin"), (T.x[:], []), 2.0)
+    dma("sa", B("arI"), (T.ar[:], []), 0.2)
+    dma("sa", B("uin"), (T.u[:], []), 1.0)
+    dma("sa", (T["q_w"][:].bitcast(dt.uint8), ["q_w"]), (T.wc[:], []), 2.0)
+    dma("sa", B("s_w"), (T.ws[:], []), 0.5)
+    dma("sa", B("vin"), (T.v[:], []), 1.0)
+
+    vmem(B("half"), 0.5)
     vmem(B("mpF"), 0.0)
+    vmem(B("zero"), 0.0)
     iota(B("pI"), [[0, 1]], 0, 1, False)
     iota(B("i42"), [[16, 2], [0, 2]])
     iota(B("ramp"), [[1, 288]])
-    idn = B("ident")
-    on = B("ones")
-    op("g", on[1], idn[1], lambda e: e.affine_select(idn[0], on[0], [[-1, 128]], OP.is_equal, 0.0, 0, 1))
+    for b in range(4):
+        eb, on = B("et", 512 * b, 512 * b + 512, key="et%d" % b), B("half")
+        op("g", on[1], eb[1], lambda e, q, b=b, eb=eb, on=on: e.affine_select(eb[0], on[0], [[-8, 128], [1, 4]], OP.is_equal, 0.0, -b, 8), 1.2)
     iota(B("upI"), [[1, 4], [64, 2]])
-    iota(B("lrI"), [[8, 2]], 2)
-    iota(B("pl"), [[-2, 2], [0, 2]], 2)
+    iota(B("lrI"), [[4, 2]], 1)
+    iota(B("pl"), [[-1, 2], [0, 2]], 1)
     iota(B("i8"), [[16, 8]])
     iota(B("k288"), [[0, 4], [288, 4], [0, 2]])
     iota(B("cG"), [[576, 4], [0, 4], [288, 2]], -NONE)
@@ -261,148 +303,118 @@ def rank_program(g, core, T, topo):
     iota(B("K2", 32, 64), [[0, 8], [1, 2], [0, 2]])
     iota(B("e16"), [[0, 8], [1, 16]])
 
-    def ci(c, sh, an):
-        o, i = B("cI", c, c + 1), B("pI")
+    def bits(c, sh, an):
+        o, i = B("cI", c, c + 1, key="cI%d" % c), B("pI")
         if sh and an:
             vts(o, i, sh, OP.logical_shift_right, an, OP.bitwise_and)
         elif sh:
             vts(o, i, sh, OP.logical_shift_right)
         else:
             vts(o, i, an, OP.bitwise_and)
+        vcopy(cf(c), o)
 
     def cf(c):
-        return B("cF", c, c + 1)
+        return B("cF", c, c + 1, key="cF%d" % c)
     for c, (sh, an) in enumerate(((0, 15), (0, 111), (3, 1), (0, 1), (4, 1), (2, 1), (1, 1), (6, 1), (5, 1), (4, 0))):
-        ci(c, sh, an)
-    vcopy(B("cF", 10, 11), B("pI"))
-    vcopy(B("cF", 0, 10), B("cI", 0, 10))
+        bits(c, sh, an)
+    vcopy(cf(10), B("pI"))
     vts(B("dupu"), B("i42"), cf(0), OP.add)
-    vts(B("offa", 0, 4), B("i42"), cf(1), OP.add)
-    vts(B("AQ", 0, 2, key="AQa"), B("i42", 0, 4, 2), cf(1), OP.add)
-    vmem(B("et"), 0.0)
-    for b in range(4):
-        acopy(B("et", 512 * b + b, 512 * b + 512, 4), B("ident"), 0.5)
+    vts(B("offa"), B("i42"), cf(1), OP.add)
+    vts(B("AQ", 0, 10, 9, key="AQa"), B("i42", 0, 4, 2), cf(1), OP.add)
+    quant("eh", B("et", key=["et0", "et1", "et2", "et3"]))
 
     vcopy(B("mpF", 0, 18), B("mpI"))
     vtr(B("U0"), B("mpF"))
     vcopy(B("U1"), IND(B("U0"), B("dupu")))
     vtr(B("U2"), B("U1"))
-    vcopy(B("U3", 0, 18, key="U3a"), B("U2", 0, 18))
-    acopy(B("U3", 18, 36, key="U3b"), B("U2", 32, 50))
+    flex("va", B("U3", 0, 18, key="U3a"), B("U2", 0, 18))
+    flex("va", B("U3", 18, 36, key="U3b"), B("U2", 32, 50))
 
-    def spread(dst, w, src, s0, skeys, engines):
-        n = 0
+    def spread(dst, w, src, s0, skeys):
+        ks = []
         for a in range(4):
-            for d in (0, 1):
-                e = a ^ d
-                copy(engines[n % len(engines)], B(dst, w * a, w * a + w, p0=32 * e, p1=32 * e + 32, key="%s.%d.%d" % (dst, a, e)),
-                     B(src, s0, s0 + w, p0=32 * a, p1=32 * a + 32, key=skeys))
-                n += 1
+            for e in (a, a ^ 1):
+                ks.append("%s.%d.%d" % (dst, a, e))
+                flex("va", B(dst, w * a, w * a + w, p0=32 * e, p1=32 * e + 32, key=ks[-1]), B(src, s0, s0 + w, p0=32 * a, p1=32 * a + 32, key=skeys))
         for h in (0, 1):
-            ks = ["%s.%d.%d" % (dst, a, e) for a in (2 * h, 2 * h + 1) for e in (2 * h, 2 * h + 1)]
-            copy(engines[(n + h) % len(engines)], B(dst, 2 * w * h, 2 * w * h + 2 * w, p0=64 - 64 * h, p1=128 - 64 * h, key="%s.h%d" % (dst, h)),
-                 B(dst, 2 * w * h, 2 * w * h + 2 * w, p0=64 * h, p1=64 * h + 64, key=ks))
-        return ["%s.%d.%d" % (dst, a, a ^ d) for a in range(4) for d in (0, 1)] + [dst + ".h0", dst + ".h1"]
+            k2 = ["%s.%d.%d" % (dst, a, e) for a in (2 * h, 2 * h + 1) for e in (2 * h, 2 * h + 1)]
+            ks.append("%s.h%d" % (dst, h))
+            flex("va", B(dst, 2 * w * h, 2 * w * h + 2 * w, p0=64 - 64 * h, p1=128 - 64 * h, key=ks[-1]),
+                 B(dst, 2 * w * h, 2 * w * h + 2 * w, p0=64 * h, p1=64 * h + 64, key=k2))
+        return ks
 
-    alk = spread("AL", 36, "U3", 0, ("U3a", "U3b"), "va")
+    alk = spread("AL", 36, "U3", 0, ("U3a", "U3b"))
     vcopy(B("ALu"), B("AL", key=alk))
     for m in range(8):
-        copy("v" if m in (0, 3, 6) else "a", B("tab", C * m, C * m + C, key="t%d" % m), IND(B("ramp"), B("ALu", 18 * m, 18 * m + 18)))
+        flex("va", B("tab", C * m, C * m + C, key="t%d" % m), IND(B("ramp"), B("ALu", 18 * m, 18 * m + 18)))
     tabk = ["t%d" % m for m in range(8)]
 
-    vcopy(B("ah", 0, 1), cf(5))
-    vcopy(B("ah", 1, 2), cf(5))
+    for c, k in ((0, 5), (1, 5)):
+        vcopy(B("ah", c, c + 1), cf(k))
     vmem(B("ah", 2, 3), 0.0)
     vmem(B("ah", 3, 4), 1.0)
-    vcopy(B("al", 0, 1), cf(6))
-    vcopy(B("al", 1, 2), cf(6))
-    vcopy(B("al", 2, 3), cf(2))
-    vcopy(B("al", 3, 4), cf(2))
+    for c, k in ((0, 6), (1, 6), (2, 2), (3, 2)):
+        vcopy(B("al", c, c + 1), cf(k))
     vts(B("ah"), B("ah"), cf(7), OP.subtract)
     vts(B("al"), B("al"), cf(8), OP.subtract)
     vtt(B("xh"), B("ah"), B("ah"), OP.mult)
     vtt(B("xl"), B("al"), B("al"), OP.mult)
-    vts(B("s2", 0, 1, key="s2a"), cf(9), 2.0, OP.mult, cf(3), OP.add)
+    vts(B("s2", 0, 1, key="s2a"), cf(3), 9.0, OP.mult, cf(9), OP.add)
     vts(B("ls"), B("xh"), 36.0, OP.mult, B("s2", 0, 1, key="s2a"), OP.add)
     vts(B("xl"), B("xl"), 18.0, OP.mult)
     vtt(B("ls"), B("ls"), B("pl"), OP.add)
     vtt(B("ls2"), B("ls"), B("xl"), OP.add)
     vcopy(B("selu"), B("ls2"))
 
-    def chain(first=False):
-        for m in range(8):
-            t = B("TR", 64 * m, 64 * m + 64, key="TR%d" % m)
-            off = B("offa", 4 * m, 4 * m + 4, key="offa" if m == 0 else "of%d" % m)
-            vcopy(B("G64"), IND(B("tab", C * m, C * m + C, key="t%d" % m), off))
-            vtr(t, B("G64"))
-            two = B("TR", 64 * m + 31, 64 * m + 33, key="TR%d" % m)
-            if m < 7:
-                vcopy(B("offa", 4 * m + 4, 4 * m + 8, key="of%d" % (m + 1)), B("TR", 64 * m + 30, 64 * m + 34, key="TR%d" % m))
-                acopy(B("AQ", 2 * m + 2, 2 * m + 4, key="AQc"), two)
-            else:
-                vcopy(B("AQ", 16, 18, key="AQb"), two)
-        for a in range(4):
-            copy("va"[a % 2], B("AQ", 18, 36, p0=32 * a, p1=32 * a + 32, key="AQ1.%d" % a),
-                 B("AQ", 0, 18, p0=32 * (a ^ 1), p1=32 * (a ^ 1) + 32, key=("AQa", "AQb", "AQc")))
-        for h in (0, 1):
-            copy("va"[h], B("AQ", 36, 72, p0=64 * h, p1=64 * h + 64, key="AQ2.%d" % h),
-                 B("AQ", 0, 36, p0=64 - 64 * h, p1=128 - 64 * h, key=("AQa", "AQb", "AQc", "AQ1.%d" % (2 - 2 * h), "AQ1.%d" % (3 - 2 * h))))
-        vcopy(B("Lu"), IND(AQ, B("selu", 0, 1)))
-        vcopy(B("Lf"), IND(AQ, B("selu", 0, 1)))
-
-    AQ = B("AQ", key=("AQa", "AQb", "AQc", "AQ1.0", "AQ1.1", "AQ1.2", "AQ1.3", "AQ2.0", "AQ2.1"))
+    AQ0 = ["AQa", "AQb", "AQc0", "AQc1"]
+    AQ = B("AQ", key=AQ0 + ["AQ1.%d" % a for a in range(4)] + ["AQ2.0", "AQ2.1"])
     LL = B("Lu", 0, 8)
+
+    def chain():
+        for m in range(8):
+            vcopy(B("G64"), IND(B("tab", C * m, C * m + C, key="t%d" % m), B("TR", 64 * m - 34, 64 * m - 30, key="TR%d" % (m - 1)) if m else B("offa")))
+            vtr(B("TR", 64 * m, 64 * m + 64, key="TR%d" % m), B("G64"))
+            if m == 6:
+                for b in (0, 1):
+                    vcopy(B("AQ", 9 * b + 1, 9 * b + 8, key="AQc%d" % b), B("TR", 31 + b, 448, 64, key=["TR%d" % k for k in range(7)]))
+        vcopy(B("AQ", 8, 18, 9, key="AQb"), B("TR", 479, 481, key="TR7"))
+        for a in range(4):
+            flex("va", B("AQ", 18, 36, p0=32 * a, p1=32 * a + 32, key="AQ1.%d" % a), B("AQ", 0, 18, p0=32 * (a ^ 1), p1=32 * (a ^ 1) + 32, key=AQ0))
+        for h in (0, 1):
+            flex("va", B("AQ", 36, 72, p0=64 * h, p1=64 * h + 64, key="AQ2.%d" % h),
+                 B("AQ", 0, 36, p0=64 - 64 * h, p1=128 - 64 * h, key=AQ0 + ["AQ1.%d" % (2 - 2 * h), "AQ1.%d" % (3 - 2 * h)]))
+        vcopy(B("Lu"), IND(AQ, B("selu", 0, 1)))
 
     def fx():
         for b in range(4):
             mmx("p%d" % b, "eh", 128 * b, "x", C)
         for b in range(4):
-            o, i = B("Fh", C * b, C * b + C, key="Fh%d" % b), B("p%d" % b, 0, C)
-            copy("av"[b % 2], o, i)
+            flex("va", B("Fh", C * b, C * b + C, key="Fh%d" % b), B("p%d" % b, 0, C))
 
-    def base():
+    XK = ["XB0", "XB1", "XB2", "XB3"]
+
+    def base(after=()):
         for b in range(4):
-            acopy(B("XB", b, 4 * C, 4), B("p%d" % b, 0, C), 2.0)
+            flex("va", B("XB", b, 4 * C, 4, key=XK[b]), B("p%d" % b, 0, C), 2.0, after=after)
 
-    quant("eh", B("et"))
-    quant("x", B("xin"))
-    fx()
-    chain(True)
-    for b in range(4):
-        o, i = B("MT", b, 512, 4, key="MT%d" % b), IND(B("Fh", C * b, C * b + C, key="Fh%d" % b), LL)
-        if b % 2:
-            vts(o, i, 2.0, OP.mult)
-        else:
-            acopy(o, i, 2.0)
     MT = B("MT", key=("MT0", "MT1", "MT2", "MT3"))
 
-    def send_w():
-        dst = T.cores[(rank - STEP[2]) % N]
-        waits("g", ["q_w", "s_w"], [])
-        if topo.may_write(core, dst):
-            for k in range(2):
-                put(dst, pieces(T, "wd", core, dst, (0, 512))[k], pieces(T, "w", core, dst, (0, 512))[k], "aw")
-        else:
-            rel = relays(topo, core, dst, False)
-            for c in range(2):
-                for k in range(2):
-                    put(rel[c], pieces(T, "yw", core, dst, (0, 256))[k], pieces(T, "w", core, dst, (256 * c, 256 * c + 256))[k], "rw")
-
-    def setup_rest():
+    def setup():
         vcopy(B("aru"), B("arI"))
-        acopy(B("cand"), IND(B("ramp"), B("aru")))
+        for k in range(4):
+            flex("va", B("cand", C * k, C * k + C, key="cand%d" % k), IND(B("ramp"), B("aru", 18 * k, 18 * k + 18)), after=("q_m1",))
         vts(B("s2", 1, 2, key="s2b"), cf(2), 2.0, OP.mult, cf(3), OP.add)
-        vts(B("s2", 2, 3, key="s2c"), B("s2", 1, 2, key="s2b"), 2.0, OP.mult, cf(4), OP.add)
+        vts(B("s2", 2, 3, key="s2c"), cf(4), 9.0, OP.mult, B("s2", 1, 2, key="s2b"), OP.add)
         vts(B("s2", 3, 4, key="s2d"), B("s2", 1, 2, key="s2b"), 16.0, OP.mult)
         vts(B("upf"), B("upI"), B("s2", 3, 4, key="s2d"), OP.add)
         vcopy(B("upu"), B("upf"))
         vts(B("lrf"), B("lrI"), B("s2", 2, 3, key="s2c"), OP.add)
         vcopy(B("lru"), B("lrf"))
-        vts(B("eru"), B("lrf"), -2.0, OP.add)
+        vts(B("eru"), B("lrf"), -1.0, OP.add)
         quant("u", B("uin"))
-        vcopy((T["q_up"][:, 0:128].bitcast(dt.uint32), ["q_up"]), (T["q_u"][:, 0:128].bitcast(dt.uint32).indirect(B("upu")[0]), ["q_u", "upu"]))
-        vcopy(B("s_up"), IND(B("s_u"), B("upu")))
-        vts(B("cG"), B("cG"), 255.5 / 512, OP.subtract)
+        up = B("upu")
+        op("v", ["q_u", "upu"], ["q_up"], lambda e, q: e.tensor_copy(T["q_up"][:, 0:128].bitcast(dt.uint32), T["q_u"][:, 0:128].bitcast(dt.uint32).indirect(up[0])), 0.25)
+        flex("va", B("s_up"), IND(B("s_u"), up))
         vts(B("jrl"), B("i8"), cf(0), OP.add)
         vts(B("mask16"), B("e16"), cf(0), OP.is_equal)
         vts(B("seg"), B("e16"), 0.0, OP.is_gt)
@@ -411,178 +423,197 @@ def rank_program(g, core, T, topo):
         vts(B("park2"), B("jrl"), float(C), OP.add)
         vts(B("jfr"), B("ramp", 0, 128), 1.0 / 256, OP.mult)
         vts(B("jcp"), cf(10), 1.0 / 256, OP.mult)
-        vmem(B("mg"), MAGIC)
-        vmem(B("nmg"), -MAGIC)
-
-    def setup_late():
-        acopy(B("et1"), B("et"), 2.0)
-        quant("e1", B("et1"))
+        for b in range(4):
+            flex("a", B("et1", 512 * b, 512 * b + 512, key="eu%d" % b), B("et", 512 * b, 512 * b + 512, key="et%d" % b), 2.0, after=("q_m1",))
+        quant("e1", B("et1", key=["eu0", "eu1", "eu2", "eu3"]))
         quant("v", B("vin"))
 
     def asks():
         vtt(B("oc1"), IND(AQ, B("selu", 2, 4)), B("k288"), OP.add)
         vcopy(B("ocu"), B("oc1"))
-        acopy(B("AN", 0, 256, key="AN0"), IND(B("cand"), B("ocu", 0, 16)))
-        vcopy(B("AN", 256, 512, key="AN1"), IND(B("cand"), B("ocu", 16, 32)))
-        vtr(B("AT", 256, 512, key="AT1"), B("AN", 256, 512, key="AN1"))
-        vtr(B("AT", 0, 256, key="AT0"), B("AN", 0, 256, key="AN0"))
+        for h in (0, 1):
+            flex("va", B("AN", 256 * h, 256 * h + 256, key="AN%d" % h), IND(B("cand", key=["cand0", "cand1", "cand2", "cand3"]), B("ocu", 16 * h, 16 * h + 16)))
+            vtr(B("AT", 256 * h, 256 * h + 256, key="AT%d" % h), B("AN", 256 * h, 256 * h + 256, key="AN%d" % h))
         ks = []
-        for a in (2, 3, 0, 1):
+        for a in range(4):
             for b in range(4):
-                k = "AC.%d.%d" % (a, b)
-                ks.append(k)
-                copy("va"[b % 2], B("AC", 8 * b, 8 * b + 8, p0=32 * a, p1=32 * a + 32, key=k),
+                ks.append("AC.%d.%d" % (a, b))
+                flex("va", B("AC", 8 * b, 8 * b + 8, p0=32 * a, p1=32 * a + 32, key=ks[-1]),
                      B("AT", 128 * a, 128 * a + 128, 16, p0=32 * b, p1=32 * b + 32, key="AT%d" % (a // 2)))
         AC = B("AC", key=ks)
         vtt(B("wr"), IND(AQ, B("lru")), AC, OP.not_equal)
         vtt(B("e1"), IND(AQ, B("eru")), B("cG"), OP.add)
-        vts(B("a5"), AC, 1.0 / 512, OP.mult)
+        vts(B("a5"), AC, 1.0 / 512, OP.mult, -255.5 / 512, OP.add)
         vtt(B("r1"), B("e1"), B("a5"), OP.add)
-        vtt(B("R"), B("r1"), B("wr"), OP.mult)
-
-    def serve(t):
-        dst = T.cores[(rank - STEP[t - 1]) % N]
-        lay("w", "lm%d" % t, "h%d" % t)
-        send("h%d" % t, dst)
+        vtt(B("KR", 0, 32, key="KR0"), B("e1"), B("wr"), OP.mult)
+        vtt(B("KR", 32, 64, key="KR1"), B("r1"), B("wr"), OP.mult)
 
     def lay(w, m, h):
         for b in range(4):
             mmx("p%d" % (4 + b), w, 128 * b, m, 128)
         for b in range(4):
-            o, i = B("HT", b, 512, 4, key="HT%d" % b), B("p%d" % (4 + b), 0, 128)
-            if b % 2:
-                vts(o, i, 0.0, OP.max, 0.03125, OP.mult)
-            else:
-                acopy(o, i, 0.03125, AF.Relu)
+            flex("va", B("HT", b, 512, 4, key="HT%d" % b), B("p%d" % (4 + b), 0, 128), 0.03125, relu=True)
         quant(h, B("HT", key=("HT0", "HT1", "HT2", "HT3")))
 
-    def least(comb, nt, m):
+    def least(comb, ck, nt, m):
         for c in range(8):
             n = 16 * c + 16
-            d, i, bi = B("DD", 128 * c, 128 * c + n, key="DD%d" % c), B(comb[0], 0, n, key=comb[1]), B(nt, c, c + 1)
-            op("a", i[1] + bi[1], d[1], lambda e, d=d, i=i, bi=bi: e.activation(d[0], i[0], AF.Identity, bias=bi[0]))
-        for c in range(8):
-            n = 16 * c + 16
-            d, o = B("DD", 128 * c, 128 * c + n, key="DD%d" % c), B(m, c, c + 1)
-            op("v", d[1], o[1], lambda e, d=d, o=o: e.tensor_reduce(o[0], d[0], AxisListType.X, OP.min, apply_absolute_value=True))
-
-    def scores(h):
-        mmx("p4", h, 0, "up", 128)
+            d = B("DD", 128 * c, 128 * c + n, key="DD%d" % c)
+            flex("va", d, B(comb, 0, n, key=ck), bias=B(nt, c, c + 1))
+            vmin(B(m, c, c + 1, key="%s.%d" % (m, c)), d, True)
 
     def halves(h):
         for b in range(4):
             mmx("p%d" % b, "eh", 128 * b, h, 128)
-        for b in range(4):
-            acopy(B("Hh", 128 * b, 128 * b + 128, key="Hh%d" % b), B("p%d" % b, 0, 128))
+        for b in (0, 1):
+            flex("va", B("Hh", 128 * b, 128 * b + 128, key="Hh%d" % b), B("p%d" % b, 0, 128))
+
+    MK, M2 = B("mm", key=["mm.%d" % c for c in range(8)]), B("m2", key=["m2.%d" % c for c in range(8)])
 
     def repair():
         vts(B("G2"), B("p4", 0, 64), 0.0, OP.is_gt)
         vtt(B("Q2"), B("G2"), B("K2"), OP.is_equal)
         vtt(B("q3"), B("Q2", 0, 32), B("Q2", 32, 64), OP.mult)
-        vtt(B("q4"), B("q3"), B("R"), OP.mult)
-        o, i = B("r"), B("q4")
-        op("v", i[1], o[1], lambda e: e.tensor_reduce(o[0], i[0], AxisListType.X, OP.min))
-        vts(B("km"), B("r"), MAGIC, OP.add)
-        vts(B("X64", 0, 32), B("nmg"), B("km"), OP.add, B("jcp"), OP.add)
-        vts(B("X64", 32, 64), B("mg"), B("km"), OP.subtract, B("r"), OP.add)
-        vtr(B("XT"), B("X64"))
-        fck = spread("FC", 32, "XT", 0, "XT", "va")
-        FC = B("FC", key=fck)
-        vtt(B("mk"), FC, B("mask16"), OP.mult)
-        fak = spread("FA", 32, "XT", 32, "XT", "a")
+        for h in (0, 1):
+            vtt(B("q4", 32 * h, 32 * h + 32, key="q4%d" % h), B("q3"), B("KR", 32 * h, 32 * h + 32, key="KR%d" % h), OP.mult)
+            vmin(B("rk", h, h + 1, key="rk%d" % h), B("q4", 32 * h, 32 * h + 32, key="q4%d" % h))
+        k, r = B("rk", 0, 1, key="rk0"), B("rk", 1, 2, key="rk1")
+        vts(B("X64", 0, 32, key="X0"), B("zero"), k, OP.add, B("jcp"), OP.add)
+        vts(B("X64", 32, 64, key="X1"), B("zero"), r, OP.add, k, OP.subtract)
+        vtr(B("XT"), B("X64", key=("X0", "X1")))
+        fck = spread("FC", 32, "XT", 0, "XT")
+        fak = spread("FA", 32, "XT", 32, "XT")
+        vtt(B("mk"), B("FC", key=fck), B("mask16"), OP.mult)
         sg, mk, sc = B("seg"), B("mk"), B("scn")
-        op("v", sg[1] + mk[1], sc[1], lambda e: e.tensor_tensor_scan(sc[0], sg[0], mk[0], 0.0, OP.mult, OP.add))
+        op("v", sg[1] + mk[1], sc[1], lambda e, q: e.tensor_tensor_scan(sc[0], sg[0], mk[0], 0.0, OP.mult, OP.add), 0.13)
         vtt(B("nt"), B("jf"), B("scn", 15, 128, 16), OP.subtract)
         vts(B("krl"), B("nt"), -1.0, OP.mult, float(NONE), OP.add)
-        least(("FC", fck), "nt", "mm")
-        FA, aD = B("FA", key=fak), B("aD")
-        op("a", FA[1], aD[1], lambda e: e.activation(aD[0], FA[0], AF.Copy, bias=255.5, scale=512.0))
-        vtt(B("lo"), B("mm"), B("jf"), OP.not_equal)
+        least("FC", fck, "nt", "mm")
+        FA, aD, ou = B("FA", key=fak), B("aD"), B("ou")
+        op("a", FA[1], aD[1], lambda e, q: e.activation(aD[0], FA[0], AF.Copy, bias=255.5, scale=512.0), 0.13)
+        vtt(B("lo"), MK, B("jf"), OP.not_equal)
         vtt(B("e2"), B("lo"), B("park"), OP.mult)
         vtt(B("o2"), B("e2"), B("krl"), OP.max)
-        vcopy(B("ou"), B("o2"))
-        op("v", aD[1] + ["ou"] + tabk, tabk, lambda e: e.tensor_copy(T["tab"][:, 0:TAB].indirect(B("ou")[0]), aD[0]))
+        vcopy(ou, B("o2"))
+        op("v", aD[1] + ou[1] + tabk, tabk, lambda e, q: e.tensor_copy(T["tab"][:, 0:TAB].indirect(ou[0]), aD[0]), 0.53)
 
     def means():
+        vts(B("nt2"), IND(AQ, B("selu", 0, 1)), -1.0, OP.mult)
         vtt(B("cb"), IND(B("ramp"), LL), B("jfr"), OP.add)
-        vts(B("nt2"), B("Lf"), -1.0, OP.mult)
-        for b in range(4):
-            vtt(B("ZT", b, 512, 4), IND(B("Fh", C * b, C * b + C, key="Fh%d" % b), LL), B("Hh", 128 * b, 128 * b + 128, key="Hh%d" % b), OP.add)
+        for b in (2, 3):
+            flex("a", B("FL", 128 * b - 256, 128 * b - 128, key="FL%d" % b), IND(B("Fh", C * b, C * b + C, key="Fh%d" % b), LL))
+        for b in (0, 1):
+            vtt(B("ZT", b, 512, 4, key="ZT%d" % b), IND(B("Fh", C * b, C * b + C, key="Fh%d" % b), LL), B("Hh", 128 * b, 128 * b + 128, key="Hh%d" % b), OP.add)
+        for b in (2, 3):
+            vtt(B("ZT", b, 512, 4, key="ZT%d" % b), B("FL", 128 * b - 256, 128 * b - 128, key="FL%d" % b), B("p%d" % b, 0, 128), OP.add)
+        least("cb", "cb", "nt2", "m2")
+
+    ZT = B("ZT", key=["ZT%d" % b for b in range(4)])
 
     def state():
-        vtt(B("lo2"), B("m2"), B("jf"), OP.not_equal)
+        vts(B("Lf"), B("nt2"), -1.0, OP.mult)
+        vtt(B("lo2"), M2, B("jf"), OP.not_equal)
         vtt(B("e3"), B("lo2"), B("park2"), OP.mult)
         vtt(B("o3"), B("e3"), B("Lf", 0, 8), OP.max)
         for t in range(4):
-            vts(B("XLu", 8 * t, 8 * t + 8, key="XL%d" % t), B("o3"), 4.0, OP.mult, float(t), OP.add)
-        for t in range(4):
-            op("v", ["ZT", "XL%d" % t, "XB"], ["XB"], lambda e, t=t: e.tensor_copy(T["XB"][:, 0:XPAD].indirect(B("XLu", 8 * t, 8 * t + 8)[0]), T["ZT"][:, t:512:4]))
-        quant("x", B("XB", 0, 4 * C))
+            xl = B("XLu", 8 * t, 8 * t + 8, key="XL%d" % t)
+            vts(xl, B("o3"), 4.0, OP.mult, float(t), OP.add)
+            op("v", ["ZT%d" % t, "XL%d" % t] + XK, XK, lambda e, q, t=t, xl=xl: e.tensor_copy(T["XB"][:, 0:XPAD].indirect(xl[0]), T["ZT"][:, t:512:4]), 0.53)
+        quant("x", B("XB", 0, 4 * C, key=XK))
 
     def next_m(tag):
-        quant("z", B("ZT"))
+        quant("z", ZT)
         for b in range(4):
             mmx("p%d" % (4 + b), "e1", 128 * b, "z", 128)
-        least(("cb", "cb"), "nt2", "m2")
-        vts(B("jm"), B("m2"), 256.0, OP.mult)
         for b in range(4):
-            acopy(B("ZD", 128 * b, 128 * b + 128, key="ZD%d" % b), B("p%d" % (4 + b), 0, 128))
+            flex("va", B("ZD", 128 * b, 128 * b + 128, key="ZD%d" % b), B("p%d" % (4 + b), 0, 128))
+        vts(B("jm"), M2, 256.0, OP.mult)
         for b in range(4):
-            copy("av"[b % 2], B("MT", b, 512, 4, key="MT%d" % b), IND(B("ZD", 128 * b, 128 * b + 128, key="ZD%d" % b), B("jm")))
+            flex("va", B("MT", b, 512, 4, key="MT%d" % b), IND(B("ZD", 128 * b, 128 * b + 128, key="ZD%d" % b), B("jm")))
         quant(tag, MT)
 
-    donor = [T.cores[(rank + s) % N] for s in STEP]
-    asker = [T.cores[(rank - s) % N] for s in STEP]
-    for t in (1, 2):
-        arrive("am%d" % t, arrival_count(asker[t - 1], core, True, 2), ["q_lm%d" % t, "s_lm%d" % t])
-        arrive("ah%d" % t, arrival_count(donor[t - 1], core, True, 2), ["q_lh%d" % t, "s_lh%d" % t])
-    arrive("aw", arrival_count(donor[2], core, False, 2 if topo.may_write(donor[2], core) else 4), ["q_wd", "s_wd"])
-
+    quant("x", B("xin"))
+    fx()
+    chain()
+    for b in range(4):
+        flex("va", B("MT", b, 512, 4, key="MT%d" % b), IND(B("Fh", C * b, C * b + C, key="Fh%d" % b), LL), 2.0)
     quant("m1", MT)
-    send("m1", donor[0])
-    send_w()
-    setup_rest()
+    base(("q_m1",))
+    setup()
     asks()
-    serve(1)
-    base()
-    setup_late()
-    scores("lh1")
-    halves("lh1")
-    repair()
-    chain()
-    means()
-    next_m("m2")
-    send("m2", donor[1])
-    asks()
-    serve(2)
-    state()
-    fx()
-    base()
-    scores("lh2")
-    halves("lh2")
-    repair()
-    chain()
-    means()
-    next_m("m3")
+    for t in (1, 2):
+        send("m%d" % t, donor[t - 1])
+        if t == 1:
+            send_w()
+            arrive("aw", donor[2], False, 2 if topo.may_write(donor[2], core) else 4, "out_w", "wd")
+        arrive("am%d" % t, asker[t - 1], True, 2, "out_m%d" % t, "lm%d" % t)
+        lay("w", "lm%d" % t, "h%d" % t)
+        send("h%d" % t, asker[t - 1])
+        if t == 2:
+            asks()
+            state()
+            fx()
+            base()
+        arrive("ah%d" % t, donor[t - 1], True, 2, "out_h%d" % t, "lh%d" % t)
+        mmx("p4", "lh%d" % t, 0, "up", 128)
+        halves("lh%d" % t)
+        repair()
+        chain()
+        means()
+        next_m("m%d" % (t + 1))
     lay("wd", "m3", "h3")
-    scores("h3")
     asks()
     state()
     fx()
     base()
+    mmx("p4", "h3", 0, "up", 128)
     halves("h3")
     repair()
-    dma("s", (T.fo[:], []), B("tab", 0, NONE, p0=0, p1=1, key=tabk))
+    dma("s", (T.fo[:], []), B("tab", 0, NONE, p0=0, p1=1, key=tabk), 0.1)
     chain()
     means()
-    least(("cb", "cb"), "nt2", "m2")
     state()
     mmx("p4", "v", 0, "x", C)
-    acopy(B("ysb"), B("p4", 0, C))
-    dma("s", (T.oc[:], []), (T["q_x"][:, 0:C].bitcast(dt.uint8), ["q_x"]))
+    flex("va", B("ysb"), B("p4", 0, C))
+    dma("sa", (T.oc[:], []), (T["q_x"][:, 0:C].bitcast(dt.uint8), ["q_x"]), 1.0)
     for k in range(4):
-        dma("s", (T.osc[4 * k:4 * k + 4, :], []), (T["s_x"][32 * k:32 * k + 4, 0:C], ["s_x"]))
-    dma("a", (T.y[:], []), B("ysb"))
+        dma("sa", (T.osc[4 * k:4 * k + 4, :], []), (T["s_x"][32 * k:32 * k + 4, 0:C], ["s_x"]), 0.1)
+    dma("sa", (T.y[:], []), B("ysb"), 1.0)
+
+    preds = depend(nodes)
+    _, order, where = min((schedule(nodes, preds, s, v, e) for s in (0.2, 0.3, 0.5) for v in (0.03, 0.06, 0.1, 0.15) for e in (0.0, 0.03)), key=lambda r: r[0])
+    eng = {"v": g.vector, "a": g.scalar, "p": g.tensor, "g": g, "s": g.sync}
+    csem = {"v": "cv", "a": "ca", "p": "cp", "g": "cg"}
+    cnt, clock, token, ndma = {}, {q: {} for q in eng}, {}, 0
+    for i in order:
+        qs, rd, wr, fn, _, kind = nodes[i]
+        if kind[0] == "arr":
+            cnt[kind[2]] = cnt.get(kind[2], 0) + fn
+            token[i] = (kind[2], cnt[kind[2]], {kind[2]: cnt[kind[2]]})
+            continue
+        q = where[i]
+        need = [token[j] for j, raw in preds[i].items() if j in token and (raw or where[j] != q or nodes[j][5][0] != "op")]
+        for sem, lev, snap in sorted(need, key=lambda t: -t[1]):
+            if clock[q].get(sem, 0) < lev:
+                eng[q].wait_ge(T.sem[sem], lev)
+                for a, b in snap.items():
+                    clock[q][a] = max(b, clock[q].get(a, 0))
+        snap = dict(clock[q])
+        if kind[0] == "send":
+            for dst, out, inp, sem in fn:
+                rid, pid = topo.addr(dst, core)
+                g.remote_dma(out, inp, T.sem[sem], T.sem["sent"], pid, rid, topo.mask(core, dst))
+                cnt["sent"] = cnt.get("sent", 0) + len(topo.engines(core, dst))
+            continue
+        if kind[0] == "dma":
+            sem, n, ins = "d%d" % ndma, 16, eng[q].dma_start(fn[0], fn[1])
+            ndma += 1
+        else:
+            sem, n, ins = csem[q], 1, fn(eng[q], q)
+        ins.then_inc(T.sem[sem], n)
+        cnt[sem] = cnt.get(sem, 0) + n
+        snap[sem] = cnt[sem]
+        token[i] = (sem, cnt[sem], snap)
     for sem in cnt:
-        if cnt[sem] and clock["g"].get(sem, 0) < cnt[sem]:
+        if clock["g"].get(sem, 0) < cnt[sem]:
             g.wait_ge(T.sem[sem], cnt[sem])

from concourse.mybir import dt, AluOpType as OP, AxisListType, ActivationFunctionType as AF

N, C, J = 8, 288, 128
STEP = [1, 2, 4]
NONE = 2304
PARK = 2320
TAB = PARK + J
XPAD = 4 * (C + J)

F32, BF, I32, U16, Q8, U8 = "float32", "bfloat16", "int32", "uint16", "float8_e4m3fn_x4", "uint8"
_S = {
    "ramp": ([128, 288], F32), "half": ([128, 512], BF), "FL": ([128, 256], BF), "et": ([128, 2048], BF), "et1": ([128, 2048], BF),
    "pI": ([128, 1], I32), "cI": ([128, 16], I32), "cF": ([128, 16], F32), "i42": ([128, 4], F32), "e16": ([128, 128], F32),
    "mask16": ([128, 128], F32), "seg": ([128, 128], F32), "i8": ([128, 8], F32), "upI": ([128, 8], F32), "cG": ([128, 32], F32),
    "k288": ([128, 32], F32), "K2": ([128, 64], F32), "lrI": ([128, 2], F32), "pl": ([128, 4], F32), "jfr": ([128, 128], F32),
    "jrl": ([128, 8], F32), "jf": ([128, 8], F32), "park": ([128, 8], F32), "park2": ([128, 8], F32), "jcp": ([128, 1], F32),
    "zero": ([128, 32], F32), "ah": ([128, 4], F32), "al": ([128, 4], F32), "xh": ([128, 4], F32),
    "xl": ([128, 4], F32), "ls": ([128, 4], F32), "ls2": ([128, 4], F32), "s2": ([128, 4], F32), "lrf": ([128, 2], F32), "upf": ([128, 8], F32),
    "dupu": ([128, 4], U16), "selu": ([128, 4], U16), "upu": ([128, 8], U16), "lru": ([128, 2], U16), "eru": ([128, 2], U16),
    "offa": ([128, 4], U16), "mpI": ([128, 18], I32), "mpF": ([128, 32], F32), "U0": ([128, 32], F32), "U1": ([128, 64], F32),
    "U2": ([128, 64], F32), "U3": ([128, 36], F32), "AL": ([128, 144], F32), "ALu": ([128, 144], U16), "tab": ([128, TAB], F32),
    "arI": ([128, 72], I32), "aru": ([128, 72], U16), "cand": ([128, 1152], F32),
    "xin": ([128, 1152], BF), "uin": ([128, 512], BF), "vin": ([128, 512], BF),
    "G64": ([128, 64], U16), "TR": ([128, 512], U16), "AQ": ([128, 72], F32), "Lu": ([128, 16], U16), "Lf": ([128, 16], F32),
    "Fh": ([128, 1152], BF), "XB": ([128, XPAD], BF), "MT": ([128, 512], BF), "ZT": ([128, 512], BF), "ZD": ([128, 512], BF),
    "HT": ([128, 512], BF), "Hh": ([128, 512], BF), "oc1": ([128, 32], F32), "ocu": ([128, 32], U16), "AN": ([128, 512], F32),
    "AT": ([128, 512], F32), "AC": ([128, 32], F32), "wr": ([128, 32], F32), "e1": ([128, 32], F32), "a5": ([128, 32], F32),
    "r1": ([128, 32], F32), "KR": ([128, 64], F32), "G2": ([128, 64], F32), "Q2": ([128, 64], F32), "q3": ([128, 32], F32),
    "q4": ([128, 64], F32), "rk": ([128, 2], F32), "X64": ([128, 64], F32), "XT": ([128, 64], F32),
    "FC": ([128, 128], F32), "FA": ([128, 128], F32), "aD": ([128, 128], F32), "mk": ([128, 128], F32), "scn": ([128, 128], F32),
    "nt": ([128, 8], F32), "krl": ([128, 8], F32), "DD": ([128, 1024], F32), "mm": ([128, 8], F32), "lo": ([128, 8], F32),
    "e2": ([128, 8], F32), "o2": ([128, 8], F32), "ou": ([128, 8], U16), "cb": ([128, 128], F32), "nt2": ([128, 16], F32),
    "m2": ([128, 8], F32), "jm": ([128, 8], U16), "lo2": ([128, 8], F32), "e3": ([128, 8], F32), "o3": ([128, 8], F32),
    "XLu": ([128, 32], U16), "ysb": ([128, 288], F32),
}
for _n, _w in (("eh", 512), ("e1", 512), ("u", 128), ("up", 128), ("v", 128), ("w", 512), ("wd", 512), ("x", 288), ("z", 128), ("m1", 128), ("m2", 128),
               ("m3", 128), ("h1", 128), ("h2", 128), ("h3", 128), ("lm1", 128), ("lm2", 128), ("lh1", 128), ("lh2", 128),
               ("ym1", 128), ("ym2", 128), ("yh1", 128), ("yh2", 128), ("yw", 256)):
    _S["q_" + _n] = ([128, _w], Q8)
    _S["s_" + _n] = ([128, _w], U8)
KIND = {k: ("b" if v[1] in (BF, U16) else "f") for k, v in _S.items()}
AT_ = {}
_PACK = {F32: ("fpack", [0]), U16: ("upack", [0])}
for _n, (_sh, _d) in list(_S.items()):
    if _d in _PACK and _sh[1] <= 128 and _n not in ("U0", "AQ"):
        _b, _o = _PACK[_d]
        AT_[_n] = (_b, _o[0], _sh[1])
        _o[0] += (_sh[1] + 7) // 8 * 8
        del _S[_n]
for _b, _d in (("fpack", F32), ("upack", U16)):
    _S[_b] = ([128, _PACK[_d][1][0]], _d)
SCRATCH = {k: ("sbuf", a, b) for k, (a, b) in _S.items()}
for _i in range(8):
    SCRATCH["p%d" % _i] = ("psum", [128, 512], F32)
NDMA = 20
SEMAPHORES = ["cv", "ca", "cp", "cg", "sent", "rw", "aw"] + ["d%d" % i for i in range(NDMA)] + [a + b for a in ("r", "a") for b in ("m1", "m2", "h1", "h2")]
PSKEYS = ["p%d" % i for i in range(8)]
WAKE = 0.08


def relays(topo, src, dst, same):
    return [c for c in topo.cores_of(src) if c != src and (topo.die(c) == topo.die(src)) == same and topo.may_write(c, dst)][:2]


def pieces(T, tag, a, b):
    return T["q_" + tag][:, a:b].bitcast(dt.uint8), T["s_" + tag][:, a:b]


def edges(T, t):
    for r in range(N):
        yield "m%d" % t, T.cores[r], T.cores[(r + STEP[t - 1]) % N]
        yield "h%d" % t, T.cores[(r + STEP[t - 1]) % N], T.cores[r]


def hand_on(g, core, T, topo):
    sent = 0
    def put(dst, out, inp, sem):
        rid, pid = topo.addr(dst, core)
        g.remote_dma(out, inp, T.sem[sem], T.sem["sent"], pid, rid, topo.mask(core, dst))
        return len(topo.engines(core, dst))
    todo = [("w", T.cores[(r + STEP[2]) % N], T.cores[r]) for r in range(N)]
    for t in (1, 2):
        e = list(edges(T, t))
        todo += [a for a in e if a[0][0] == "m"] + [a for a in e if a[0][0] == "h"]
    for tag, src, dst in todo:
        if core not in topo.cores_of(src) or topo.may_write(src, dst):
            continue
        rel = relays(topo, src, dst, tag != "w")
        if core not in rel:
            continue
        k = rel.index(core)
        n = len(topo.engines(src, core))
        if tag == "w":
            g.wait_ge(T.sem["rw"], 2 * n)
            q, s = pieces(T, "yw", 0, 256)
            q2, s2 = pieces(T, "wd", 256 * k, 256 * k + 256)
            sent += put(dst, q2, q, "aw")
            sent += put(dst, s2, s, "aw")
        else:
            g.wait_ge(T.sem["r" + tag], n)
            a, b = pieces(T, "y" + tag, 0, 128)[k], pieces(T, "l" + tag, 0, 128)[k]
            sent += put(dst, b, a, "a" + tag)
    if sent:
        g.wait_ge(T.sem["sent"], sent)


def depend(nodes):
    lastw, readers, preds = {}, {}, []
    for i, nd in enumerate(nodes):
        rd = [k for k in nd[1] if k not in PSKEYS]
        wr = list(nd[2]) + [k for k in nd[1] if k in PSKEYS]
        p = {}
        for k in nd[1]:
            if k in lastw:
                p[lastw[k]] = True
        for k in wr:
            for j in ([lastw[k]] if k in lastw else []) + readers.get(k, []):
                p.setdefault(j, False)
        p.pop(i, None)
        preds.append(p)
        for k in rd:
            readers.setdefault(k, []).append(i)
        for k in wr:
            lastw[k], readers[k] = i, []
    return preds


def schedule(nodes, preds, slack, vp, eps):
    n = len(nodes)
    succ = [[] for _ in range(n)]
    for i, p in enumerate(preds):
        for j in p:
            succ[j].append(i)
    out = [nd[5][1] for nd in nodes]
    prio = [0.0] * n
    for i in range(n - 1, -1, -1):
        prio[i] = min(nodes[i][4].values()) + out[i] + max([prio[k] + (WAKE if preds[k][i] else 0.0) for k in succ[i]] + [0.0])
    left = [len(p) for p in preds]
    ready = [i for i in range(n) if not left[i]]
    qt = {q: 0.0 for q in "gvapsx"}
    end, where, order = [0.0] * n, [None] * n, []

    def start(i, q):
        t = 0.0 if q == "x" else qt[q]
        for j, raw in preds[i].items():
            if raw or where[j] != q or nodes[j][5][0] != "op":
                t = max(t, end[j] + out[j] + WAKE)
        return t
    while ready:
        cand = []
        for i in ready:
            _, s, q = min((start(i, q) + nodes[i][4][q] + (vp if q == "v" else 0.0), start(i, q), q) for q in nodes[i][0])
            cand.append((s, q, i))
        s0, q0, i0 = min(cand)
        s, q, i = min((c for c in cand if c[1] == q0 and c[0] <= s0 + slack), key=lambda c: (-prio[c[2]], c[2]))
        fit = [c for c in cand if c[1] == q0 and c[0] + nodes[c[2]][4][q0] <= s + eps and prio[c[2]] < prio[i]]
        if fit:
            s, q, i = min(fit, key=lambda c: (-prio[c[2]], c[2]))
        where[i], end[i] = q, s + nodes[i][4][q]
        if q != "x":
            qt[q] = end[i]
        order.append(i)
        ready.remove(i)
        for k in succ[i]:
            left[k] -= 1
            if not left[k]:
                ready.append(k)
    return max(end), order, where


def rank_program(g, core, T, topo):
    rank = T.rank_of(core)
    if rank is None:
        hand_on(g, core, T, topo)
        return
    nodes = []
    donor = [T.cores[(rank + s) % N] for s in STEP]
    asker = [T.cores[(rank - s) % N] for s in STEP]

    def op(qs, rd, wr, fn, cost):
        nodes.append([qs, list(rd), list(wr), fn, cost if isinstance(cost, dict) else {q: cost for q in qs}, ("op", 0.0)])

    def B(name, a=None, b=None, st=None, p0=0, p1=128, key=None):
        k = [name] if key is None else ([key] if isinstance(key, str) else list(key))
        buf, o, w = AT_[name] if name in AT_ else (name, 0, T[name].shape[1])
        lo, hi = o + (a or 0), o + (w if b is None else b)
        kind = "p" if name in PSKEYS else KIND[name]
        if st:
            return T[buf][p0:p1, lo:hi:st], k, -(-(hi - lo) // st), kind
        return T[buf][p0:p1, lo:hi], k, hi - lo, kind

    def IND(win, off):
        return win[0].indirect(off[0]), win[1] + off[1], 16 * off[2], "i"

    def X(o):
        return o if isinstance(o, tuple) else (o, [], 0, "f")

    def cost(q, o, ins, per=1.0):
        n = max([o[2]] + [i[2] for i in ins])
        if any(i[3] == "i" for i in ins):
            return (0.05 if q == "v" else 0.065) + 0.0015 * n
        if q == "v" and all(i[3] == "b" for i in list(ins) + [o]) and per == 1.0:
            per = 0.5
        return 0.001 * max(64, n * per)

    def flex(qs, o, i, scale=1.0, bias=None, relu=False, after=()):
        bi = X(bias)
        def fn(e, q):
            if q == "a":
                f = AF.Relu if relu else (AF.Copy if bias is None else AF.Identity)
                if bias is None and scale == 1.0:
                    return e.activation(o[0], i[0], f)
                return e.activation(o[0], i[0], f, scale=scale) if bias is None else e.activation(o[0], i[0], f, bias=bi[0], scale=scale)
            if relu:
                return e.tensor_scalar(o[0], i[0], 0.0, scale, OP.max, OP.mult)
            if bias is None:
                return e.tensor_copy(o[0], i[0]) if scale == 1.0 else e.tensor_scalar(o[0], i[0], scale, None, OP.mult)
            return e.tensor_scalar(o[0], i[0], bi[0], None, OP.add)
        op(qs, i[1] + bi[1] + list(after), o[1], fn, {q: cost(q, o, [i]) for q in qs})

    def vcopy(o, i):
        op("v", i[1], o[1], lambda e, q: e.tensor_copy(o[0], i[0]), cost("v", o, [i]))

    def vts(o, i, s1, op0, s2=None, op1=None):
        a, b = X(s1), X(s2)
        if op1 is None:
            op("v", i[1] + a[1], o[1], lambda e, q: e.tensor_scalar(o[0], i[0], a[0], None, op0), cost("v", o, [i]))
        else:
            op("v", i[1] + a[1] + b[1], o[1], lambda e, q: e.tensor_scalar(o[0], i[0], a[0], b[0], op0, op1), cost("v", o, [i]))

    def vtt(o, i, j, o_):
        op("v", i[1] + j[1], o[1], lambda e, q: e.tensor_tensor(o[0], i[0], j[0], o_), cost("v", o, [i, j], 1.01 if j[3] == "p" else 2.0))

    def vmem(o, c):
        op("v", [], o[1], lambda e, q: e.memset(o[0], c), cost("v", o, []))

    def vtr(o, i):
        op("v", i[1], o[1], lambda e, q: e.transpose(o[0], i[0]), cost("v", o, [i]))

    def vmin(o, i, mag=False):
        op("v", i[1], o[1], lambda e, q: e.tensor_reduce(o[0], i[0], AxisListType.X, OP.min, apply_absolute_value=mag), cost("v", o, [i]))

    def quant(tag, i):
        q_, s_ = T["q_" + tag][:], T["s_" + tag][:]
        op("v", i[1], ["q_" + tag, "s_" + tag], lambda e, q: e.quantize_mx(q_, s_, i[0]), 0.015 + 0.00027 * i[2])

    def mmx(o, l, l0, r, n):
        lq, lsc, rq, rsc = T["q_" + l][:, l0:l0 + 128], T["s_" + l][:, l0:l0 + 128], T["q_" + r][:, 0:n], T["s_" + r][:, 0:n]
        op("p", ["q_" + l, "s_" + l, "q_" + r, "s_" + r], [o], lambda e, q: e.matmul_mx(T[o][:, 0:n], lq, lsc, rq, rsc, True, True), 0.001 * (n + 16))

    def iota(o, pattern, base=0, cm=0, f=True):
        def fn(e, q):
            return e.iota(o[0], pattern, base, cm, allow_small_or_imprecise_dtypes=True) if f else e.iota(o[0], pattern, base, cm)
        op("g", [], o[1], fn, 0.15 + 0.002 * o[2])

    def dma(qs, out, inp, size):
        nodes.append([qs, list(inp[1]), list(out[1]), (out[0], inp[0]), {q: 0.08 for q in qs}, ("dma", 2.0 + size)])

    def send(tag, dst):
        src, rel = pieces(T, tag, 0, 128), None if topo.may_write(core, dst) else relays(topo, core, dst, True)
        todo = [(dst, pieces(T, "l" + tag, 0, 128)[k], src[k], "a" + tag) if rel is None else
                (rel[k], pieces(T, "y" + tag, 0, 128)[k], src[k], "r" + tag) for k in range(2)]
        nodes.append(["g", ["q_" + tag, "s_" + tag], ["out_" + tag], todo, {"g": 1.4}, ("send", 0.0)])

    def send_w():
        dst = T.cores[(rank - STEP[2]) % N]
        if topo.may_write(core, dst):
            todo = [(dst, pieces(T, "wd", 0, 512)[k], pieces(T, "w", 0, 512)[k], "aw") for k in range(2)]
        else:
            rel = relays(topo, core, dst, False)
            todo = [(rel[c], pieces(T, "yw", 0, 256)[k], pieces(T, "w", 256 * c, 256 * c + 256)[k], "rw") for c in range(2) for k in range(2)]
        nodes.append(["g", ["q_w", "s_w", "out_m1"], ["out_w"], todo, {"g": 2.8}, ("send", 0.0)])

    def arrive(tag, src, same, calls, after, lands):
        straight = topo.may_write(src, core)
        n = calls * len(topo.engines(src if straight else relays(topo, src, core, same)[0], core))
        nodes.append(["x", [after], ["q_" + lands, "s_" + lands], n, {"x": 0.0}, ("arr", 3.0 if straight else 6.0, tag)])

    dma("s", B("mpI"), (T.mp[:], []), 0.1)
    dma("s", B("xin"), (T.x[:], []), 2.0)
    dma("sa", B("arI"), (T.ar[:], []), 0.2)
    dma("sa", B("uin"), (T.u[:], []), 1.0)
    dma("sa", (T["q_w"][:].bitcast(dt.uint8), ["q_w"]), (T.wc[:], []), 2.0)
    dma("sa", B("s_w"), (T.ws[:], []), 0.5)
    dma("sa", B("vin"), (T.v[:], []), 1.0)

    vmem(B("half"), 0.5)
    vmem(B("mpF"), 0.0)
    vmem(B("zero"), 0.0)
    iota(B("pI"), [[0, 1]], 0, 1, False)
    iota(B("i42"), [[16, 2], [0, 2]])
    iota(B("ramp"), [[1, 288]])
    for b in range(4):
        eb, on = B("et", 512 * b, 512 * b + 512, key="et%d" % b), B("half")
        op("g", on[1], eb[1], lambda e, q, b=b, eb=eb, on=on: e.affine_select(eb[0], on[0], [[-8, 128], [1, 4]], OP.is_equal, 0.0, -b, 8), 1.2)
    iota(B("upI"), [[1, 4], [64, 2]])
    iota(B("lrI"), [[4, 2]], 1)
    iota(B("pl"), [[-1, 2], [0, 2]], 1)
    iota(B("i8"), [[16, 8]])
    iota(B("k288"), [[0, 4], [288, 4], [0, 2]])
    iota(B("cG"), [[576, 4], [0, 4], [288, 2]], -NONE)
    iota(B("K2", 0, 32), [[0, 4], [1, 2], [0, 4]])
    iota(B("K2", 32, 64), [[0, 8], [1, 2], [0, 2]])
    iota(B("e16"), [[0, 8], [1, 16]])

    def bits(c, sh, an):
        o, i = B("cI", c, c + 1, key="cI%d" % c), B("pI")
        if sh and an:
            vts(o, i, sh, OP.logical_shift_right, an, OP.bitwise_and)
        elif sh:
            vts(o, i, sh, OP.logical_shift_right)
        else:
            vts(o, i, an, OP.bitwise_and)
        vcopy(cf(c), o)

    def cf(c):
        return B("cF", c, c + 1, key="cF%d" % c)
    for c, (sh, an) in enumerate(((0, 15), (0, 111), (3, 1), (0, 1), (4, 1), (2, 1), (1, 1), (6, 1), (5, 1), (4, 0))):
        bits(c, sh, an)
    vcopy(cf(10), B("pI"))
    vts(B("dupu"), B("i42"), cf(0), OP.add)
    vts(B("offa"), B("i42"), cf(1), OP.add)
    vts(B("AQ", 0, 10, 9, key="AQa"), B("i42", 0, 4, 2), cf(1), OP.add)
    quant("eh", B("et", key=["et0", "et1", "et2", "et3"]))

    vcopy(B("mpF", 0, 18), B("mpI"))
    vtr(B("U0"), B("mpF"))
    vcopy(B("U1"), IND(B("U0"), B("dupu")))
    vtr(B("U2"), B("U1"))
    flex("va", B("U3", 0, 18, key="U3a"), B("U2", 0, 18))
    flex("va", B("U3", 18, 36, key="U3b"), B("U2", 32, 50))

    def spread(dst, w, src, s0, skeys):
        ks = []
        for a in range(4):
            for e in (a, a ^ 1):
                ks.append("%s.%d.%d" % (dst, a, e))
                flex("va", B(dst, w * a, w * a + w, p0=32 * e, p1=32 * e + 32, key=ks[-1]), B(src, s0, s0 + w, p0=32 * a, p1=32 * a + 32, key=skeys))
        for h in (0, 1):
            k2 = ["%s.%d.%d" % (dst, a, e) for a in (2 * h, 2 * h + 1) for e in (2 * h, 2 * h + 1)]
            ks.append("%s.h%d" % (dst, h))
            flex("va", B(dst, 2 * w * h, 2 * w * h + 2 * w, p0=64 - 64 * h, p1=128 - 64 * h, key=ks[-1]),
                 B(dst, 2 * w * h, 2 * w * h + 2 * w, p0=64 * h, p1=64 * h + 64, key=k2))
        return ks

    alk = spread("AL", 36, "U3", 0, ("U3a", "U3b"))
    vcopy(B("ALu"), B("AL", key=alk))
    for m in range(8):
        flex("va", B("tab", C * m, C * m + C, key="t%d" % m), IND(B("ramp"), B("ALu", 18 * m, 18 * m + 18)))
    tabk = ["t%d" % m for m in range(8)]

    for c, k in ((0, 5), (1, 5)):
        vcopy(B("ah", c, c + 1), cf(k))
    vmem(B("ah", 2, 3), 0.0)
    vmem(B("ah", 3, 4), 1.0)
    for c, k in ((0, 6), (1, 6), (2, 2), (3, 2)):
        vcopy(B("al", c, c + 1), cf(k))
    vts(B("ah"), B("ah"), cf(7), OP.subtract)
    vts(B("al"), B("al"), cf(8), OP.subtract)
    vtt(B("xh"), B("ah"), B("ah"), OP.mult)
    vtt(B("xl"), B("al"), B("al"), OP.mult)
    vts(B("s2", 0, 1, key="s2a"), cf(3), 9.0, OP.mult, cf(9), OP.add)
    vts(B("ls"), B("xh"), 36.0, OP.mult, B("s2", 0, 1, key="s2a"), OP.add)
    vts(B("xl"), B("xl"), 18.0, OP.mult)
    vtt(B("ls"), B("ls"), B("pl"), OP.add)
    vtt(B("ls2"), B("ls"), B("xl"), OP.add)
    vcopy(B("selu"), B("ls2"))

    AQ0 = ["AQa", "AQb", "AQc0", "AQc1"]
    AQ = B("AQ", key=AQ0 + ["AQ1.%d" % a for a in range(4)] + ["AQ2.0", "AQ2.1"])
    LL = B("Lu", 0, 8)

    def chain():
        for m in range(8):
            vcopy(B("G64"), IND(B("tab", C * m, C * m + C, key="t%d" % m), B("TR", 64 * m - 34, 64 * m - 30, key="TR%d" % (m - 1)) if m else B("offa")))
            vtr(B("TR", 64 * m, 64 * m + 64, key="TR%d" % m), B("G64"))
            if m == 6:
                for b in (0, 1):
                    vcopy(B("AQ", 9 * b + 1, 9 * b + 8, key="AQc%d" % b), B("TR", 31 + b, 448, 64, key=["TR%d" % k for k in range(7)]))
        vcopy(B("AQ", 8, 18, 9, key="AQb"), B("TR", 479, 481, key="TR7"))
        for a in range(4):
            flex("va", B("AQ", 18, 36, p0=32 * a, p1=32 * a + 32, key="AQ1.%d" % a), B("AQ", 0, 18, p0=32 * (a ^ 1), p1=32 * (a ^ 1) + 32, key=AQ0))
        for h in (0, 1):
            flex("va", B("AQ", 36, 72, p0=64 * h, p1=64 * h + 64, key="AQ2.%d" % h),
                 B("AQ", 0, 36, p0=64 - 64 * h, p1=128 - 64 * h, key=AQ0 + ["AQ1.%d" % (2 - 2 * h), "AQ1.%d" % (3 - 2 * h)]))
        vcopy(B("Lu"), IND(AQ, B("selu", 0, 1)))

    def fx():
        for b in range(4):
            mmx("p%d" % b, "eh", 128 * b, "x", C)
        for b in range(4):
            flex("va", B("Fh", C * b, C * b + C, key="Fh%d" % b), B("p%d" % b, 0, C))

    XK = ["XB0", "XB1", "XB2", "XB3"]

    def base(after=()):
        for b in range(4):
            flex("va", B("XB", b, 4 * C, 4, key=XK[b]), B("p%d" % b, 0, C), 2.0, after=after)

    MT = B("MT", key=("MT0", "MT1", "MT2", "MT3"))

    def setup():
        vcopy(B("aru"), B("arI"))
        for k in range(4):
            flex("va", B("cand", C * k, C * k + C, key="cand%d" % k), IND(B("ramp"), B("aru", 18 * k, 18 * k + 18)), after=("q_m1",))
        vts(B("s2", 1, 2, key="s2b"), cf(2), 2.0, OP.mult, cf(3), OP.add)
        vts(B("s2", 2, 3, key="s2c"), cf(4), 9.0, OP.mult, B("s2", 1, 2, key="s2b"), OP.add)
        vts(B("s2", 3, 4, key="s2d"), B("s2", 1, 2, key="s2b"), 16.0, OP.mult)
        vts(B("upf"), B("upI"), B("s2", 3, 4, key="s2d"), OP.add)
        vcopy(B("upu"), B("upf"))
        vts(B("lrf"), B("lrI"), B("s2", 2, 3, key="s2c"), OP.add)
        vcopy(B("lru"), B("lrf"))
        vts(B("eru"), B("lrf"), -1.0, OP.add)
        quant("u", B("uin"))
        up = B("upu")
        op("v", ["q_u", "upu"], ["q_up"], lambda e, q: e.tensor_copy(T["q_up"][:, 0:128].bitcast(dt.uint32), T["q_u"][:, 0:128].bitcast(dt.uint32).indirect(up[0])), 0.25)
        flex("va", B("s_up"), IND(B("s_u"), up))
        vts(B("jrl"), B("i8"), cf(0), OP.add)
        vts(B("mask16"), B("e16"), cf(0), OP.is_equal)
        vts(B("seg"), B("e16"), 0.0, OP.is_gt)
        vts(B("jf"), B("jrl"), 1.0 / 256, OP.mult)
        vts(B("park"), B("jrl"), float(PARK), OP.add)
        vts(B("park2"), B("jrl"), float(C), OP.add)
        vts(B("jfr"), B("ramp", 0, 128), 1.0 / 256, OP.mult)
        vts(B("jcp"), cf(10), 1.0 / 256, OP.mult)
        for b in range(4):
            flex("a", B("et1", 512 * b, 512 * b + 512, key="eu%d" % b), B("et", 512 * b, 512 * b + 512, key="et%d" % b), 2.0, after=("q_m1",))
        quant("e1", B("et1", key=["eu0", "eu1", "eu2", "eu3"]))
        quant("v", B("vin"))

    def asks():
        vtt(B("oc1"), IND(AQ, B("selu", 2, 4)), B("k288"), OP.add)
        vcopy(B("ocu"), B("oc1"))
        for h in (0, 1):
            flex("va", B("AN", 256 * h, 256 * h + 256, key="AN%d" % h), IND(B("cand", key=["cand0", "cand1", "cand2", "cand3"]), B("ocu", 16 * h, 16 * h + 16)))
            vtr(B("AT", 256 * h, 256 * h + 256, key="AT%d" % h), B("AN", 256 * h, 256 * h + 256, key="AN%d" % h))
        ks = []
        for a in range(4):
            for b in range(4):
                ks.append("AC.%d.%d" % (a, b))
                flex("va", B("AC", 8 * b, 8 * b + 8, p0=32 * a, p1=32 * a + 32, key=ks[-1]),
                     B("AT", 128 * a, 128 * a + 128, 16, p0=32 * b, p1=32 * b + 32, key="AT%d" % (a // 2)))
        AC = B("AC", key=ks)
        vtt(B("wr"), IND(AQ, B("lru")), AC, OP.not_equal)
        vtt(B("e1"), IND(AQ, B("eru")), B("cG"), OP.add)
        vts(B("a5"), AC, 1.0 / 512, OP.mult, -255.5 / 512, OP.add)
        vtt(B("r1"), B("e1"), B("a5"), OP.add)
        vtt(B("KR", 0, 32, key="KR0"), B("e1"), B("wr"), OP.mult)
        vtt(B("KR", 32, 64, key="KR1"), B("r1"), B("wr"), OP.mult)

    def lay(w, m, h):
        for b in range(4):
            mmx("p%d" % (4 + b), w, 128 * b, m, 128)
        for b in range(4):
            flex("va", B("HT", b, 512, 4, key="HT%d" % b), B("p%d" % (4 + b), 0, 128), 0.03125, relu=True)
        quant(h, B("HT", key=("HT0", "HT1", "HT2", "HT3")))

    def least(comb, ck, nt, m):
        for c in range(8):
            n = 16 * c + 16
            d = B("DD", 128 * c, 128 * c + n, key="DD%d" % c)
            flex("va", d, B(comb, 0, n, key=ck), bias=B(nt, c, c + 1))
            vmin(B(m, c, c + 1, key="%s.%d" % (m, c)), d, True)

    def halves(h):
        for b in range(4):
            mmx("p%d" % b, "eh", 128 * b, h, 128)
        for b in (0, 1):
            flex("va", B("Hh", 128 * b, 128 * b + 128, key="Hh%d" % b), B("p%d" % b, 0, 128))

    MK, M2 = B("mm", key=["mm.%d" % c for c in range(8)]), B("m2", key=["m2.%d" % c for c in range(8)])

    def repair():
        vts(B("G2"), B("p4", 0, 64), 0.0, OP.is_gt)
        vtt(B("Q2"), B("G2"), B("K2"), OP.is_equal)
        vtt(B("q3"), B("Q2", 0, 32), B("Q2", 32, 64), OP.mult)
        for h in (0, 1):
            vtt(B("q4", 32 * h, 32 * h + 32, key="q4%d" % h), B("q3"), B("KR", 32 * h, 32 * h + 32, key="KR%d" % h), OP.mult)
            vmin(B("rk", h, h + 1, key="rk%d" % h), B("q4", 32 * h, 32 * h + 32, key="q4%d" % h))
        k, r = B("rk", 0, 1, key="rk0"), B("rk", 1, 2, key="rk1")
        vts(B("X64", 0, 32, key="X0"), B("zero"), k, OP.add, B("jcp"), OP.add)
        vts(B("X64", 32, 64, key="X1"), B("zero"), r, OP.add, k, OP.subtract)
        vtr(B("XT"), B("X64", key=("X0", "X1")))
        fck = spread("FC", 32, "XT", 0, "XT")
        fak = spread("FA", 32, "XT", 32, "XT")
        vtt(B("mk"), B("FC", key=fck), B("mask16"), OP.mult)
        sg, mk, sc = B("seg"), B("mk"), B("scn")
        op("v", sg[1] + mk[1], sc[1], lambda e, q: e.tensor_tensor_scan(sc[0], sg[0], mk[0], 0.0, OP.mult, OP.add), 0.13)
        vtt(B("nt"), B("jf"), B("scn", 15, 128, 16), OP.subtract)
        vts(B("krl"), B("nt"), -1.0, OP.mult, float(NONE), OP.add)
        least("FC", fck, "nt", "mm")
        FA, aD, ou = B("FA", key=fak), B("aD"), B("ou")
        op("a", FA[1], aD[1], lambda e, q: e.activation(aD[0], FA[0], AF.Copy, bias=255.5, scale=512.0), 0.13)
        vtt(B("lo"), MK, B("jf"), OP.not_equal)
        vtt(B("e2"), B("lo"), B("park"), OP.mult)
        vtt(B("o2"), B("e2"), B("krl"), OP.max)
        vcopy(ou, B("o2"))
        op("v", aD[1] + ou[1] + tabk, tabk, lambda e, q: e.tensor_copy(T["tab"][:, 0:TAB].indirect(ou[0]), aD[0]), 0.53)

    def means():
        vts(B("nt2"), IND(AQ, B("selu", 0, 1)), -1.0, OP.mult)
        vtt(B("cb"), IND(B("ramp"), LL), B("jfr"), OP.add)
        for b in (2, 3):
            flex("a", B("FL", 128 * b - 256, 128 * b - 128, key="FL%d" % b), IND(B("Fh", C * b, C * b + C, key="Fh%d" % b), LL))
        for b in (0, 1):
            vtt(B("ZT", b, 512, 4, key="ZT%d" % b), IND(B("Fh", C * b, C * b + C, key="Fh%d" % b), LL), B("Hh", 128 * b, 128 * b + 128, key="Hh%d" % b), OP.add)
        for b in (2, 3):
            vtt(B("ZT", b, 512, 4, key="ZT%d" % b), B("FL", 128 * b - 256, 128 * b - 128, key="FL%d" % b), B("p%d" % b, 0, 128), OP.add)
        least("cb", "cb", "nt2", "m2")

    ZT = B("ZT", key=["ZT%d" % b for b in range(4)])

    def state():
        vts(B("Lf"), B("nt2"), -1.0, OP.mult)
        vtt(B("lo2"), M2, B("jf"), OP.not_equal)
        vtt(B("e3"), B("lo2"), B("park2"), OP.mult)
        vtt(B("o3"), B("e3"), B("Lf", 0, 8), OP.max)
        for t in range(4):
            xl = B("XLu", 8 * t, 8 * t + 8, key="XL%d" % t)
            vts(xl, B("o3"), 4.0, OP.mult, float(t), OP.add)
            op("v", ["ZT%d" % t, "XL%d" % t] + XK, XK, lambda e, q, t=t, xl=xl: e.tensor_copy(T["XB"][:, 0:XPAD].indirect(xl[0]), T["ZT"][:, t:512:4]), 0.53)
        quant("x", B("XB", 0, 4 * C, key=XK))

    def next_m(tag):
        quant("z", ZT)
        for b in range(4):
            mmx("p%d" % (4 + b), "e1", 128 * b, "z", 128)
        for b in range(4):
            flex("va", B("ZD", 128 * b, 128 * b + 128, key="ZD%d" % b), B("p%d" % (4 + b), 0, 128))
        vts(B("jm"), M2, 256.0, OP.mult)
        for b in range(4):
            flex("va", B("MT", b, 512, 4, key="MT%d" % b), IND(B("ZD", 128 * b, 128 * b + 128, key="ZD%d" % b), B("jm")))
        quant(tag, MT)

    quant("x", B("xin"))
    fx()
    chain()
    for b in range(4):
        flex("va", B("MT", b, 512, 4, key="MT%d" % b), IND(B("Fh", C * b, C * b + C, key="Fh%d" % b), LL), 2.0)
    quant("m1", MT)
    base(("q_m1",))
    setup()
    asks()
    for t in (1, 2):
        send("m%d" % t, donor[t - 1])
        if t == 1:
            send_w()
            arrive("aw", donor[2], False, 2 if topo.may_write(donor[2], core) else 4, "out_w", "wd")
        arrive("am%d" % t, asker[t - 1], True, 2, "out_m%d" % t, "lm%d" % t)
        lay("w", "lm%d" % t, "h%d" % t)
        send("h%d" % t, asker[t - 1])
        if t == 2:
            asks()
            state()
            fx()
            base()
        arrive("ah%d" % t, donor[t - 1], True, 2, "out_h%d" % t, "lh%d" % t)
        mmx("p4", "lh%d" % t, 0, "up", 128)
        halves("lh%d" % t)
        repair()
        chain()
        means()
        next_m("m%d" % (t + 1))
    lay("wd", "m3", "h3")
    asks()
    state()
    fx()
    base()
    mmx("p4", "h3", 0, "up", 128)
    halves("h3")
    repair()
    dma("s", (T.fo[:], []), B("tab", 0, NONE, p0=0, p1=1, key=tabk), 0.1)
    chain()
    means()
    state()
    mmx("p4", "v", 0, "x", C)
    flex("va", B("ysb"), B("p4", 0, C))
    dma("sa", (T.oc[:], []), (T["q_x"][:, 0:C].bitcast(dt.uint8), ["q_x"]), 1.0)
    for k in range(4):
        dma("sa", (T.osc[4 * k:4 * k + 4, :], []), (T["s_x"][32 * k:32 * k + 4, 0:C], ["s_x"]), 0.1)
    dma("sa", (T.y[:], []), B("ysb"), 1.0)

    preds = depend(nodes)
    _, order, where = min((schedule(nodes, preds, s, v, e) for s in (0.2, 0.3, 0.5) for v in (0.03, 0.06, 0.1, 0.15) for e in (0.0, 0.03)), key=lambda r: r[0])
    eng = {"v": g.vector, "a": g.scalar, "p": g.tensor, "g": g, "s": g.sync}
    csem = {"v": "cv", "a": "ca", "p": "cp", "g": "cg"}
    cnt, clock, token, ndma = {}, {q: {} for q in eng}, {}, 0
    for i in order:
        qs, rd, wr, fn, _, kind = nodes[i]
        if kind[0] == "arr":
            cnt[kind[2]] = cnt.get(kind[2], 0) + fn
            token[i] = (kind[2], cnt[kind[2]], {kind[2]: cnt[kind[2]]})
            continue
        q = where[i]
        need = [token[j] for j, raw in preds[i].items() if j in token and (raw or where[j] != q or nodes[j][5][0] != "op")]
        for sem, lev, snap in sorted(need, key=lambda t: -t[1]):
            if clock[q].get(sem, 0) < lev:
                eng[q].wait_ge(T.sem[sem], lev)
                for a, b in snap.items():
                    clock[q][a] = max(b, clock[q].get(a, 0))
        snap = dict(clock[q])
        if kind[0] == "send":
            for dst, out, inp, sem in fn:
                rid, pid = topo.addr(dst, core)
                g.remote_dma(out, inp, T.sem[sem], T.sem["sent"], pid, rid, topo.mask(core, dst))
                cnt["sent"] = cnt.get("sent", 0) + len(topo.engines(core, dst))
            continue
        if kind[0] == "dma":
            sem, n, ins = "d%d" % ndma, 16, eng[q].dma_start(fn[0], fn[1])
            ndma += 1
        else:
            sem, n, ins = csem[q], 1, fn(eng[q], q)
        ins.then_inc(T.sem[sem], n)
        cnt[sem] = cnt.get(sem, 0) + n
        snap[sem] = cnt[sem]
        token[i] = (sem, cnt[sem], snap)
    for sem in cnt:
        if clock["g"].get(sem, 0) < cnt[sem]:
            g.wait_ge(T.sem[sem], cnt[sem])
